import numpy as np
import ml_dtypes


def mxq(x, axis, fmt="e4m3"):
    dtype, down = {"e4m3": (ml_dtypes.float8_e4m3fn, 7), "e5m2": (ml_dtypes.float8_e5m2, 14)}[fmt]
    v = np.moveaxis(np.asarray(x, np.float32).astype(ml_dtypes.bfloat16).astype(np.float64), axis, -1)
    blocks = v.reshape(v.shape[:-1] + (-1, 32))
    amax = np.abs(blocks).max(-1, keepdims=True)
    byte = np.maximum(np.where(amax > 0, np.frexp(amax)[1] - 1 + 127, 0) - down, 1)
    scale = np.exp2(byte - 127.0)
    codes = (blocks / scale).astype(np.float32).astype(dtype).astype(np.float64)
    return np.moveaxis((codes * scale).reshape(v.shape), -1, axis)


WIDE = False


def mx_kscale(k):
    if not WIDE:
        return np.ones(k)
    levels = np.array([10, -10, 5, -5, 0])
    if k % 512:
        return np.exp2(np.random.permutation(np.resize(levels, k // 32))).repeat(32)
    a = np.empty((k // 512, 16))
    for p in range(k // 512):
        a[p, :8] = np.random.permutation(np.resize(levels, 8))
        for g in range(8):
            far = levels[np.abs(levels - a[p, g]) >= 10]
            a[p, g + 8] = far[np.random.randint(len(far))]
    return np.exp2(a.ravel()).repeat(32)


def f64(x):
    return np.asarray(x).astype(np.float64)


def striped(idx):
    return np.tile(idx.reshape(-1, 16).T, (8, 1)).astype(np.uint16)


def unstriped(offs):
    return offs[:16].T.reshape(-1).astype(np.int64)


def pack_weight(w):
    k, n = w.shape
    w = f64(np.asarray(w, np.float32).astype(ml_dtypes.bfloat16)).reshape(k // 32, 32, n)
    amax = np.abs(w).max(1)
    byte = np.clip(np.where(amax > 0, np.frexp(amax)[1] - 1 + 127 - 7, 1), 1, 254)
    scaled = (w * np.exp2(127.0 - byte)[:, None, :]).reshape(k, n).astype(np.float32)
    words = np.ascontiguousarray(scaled.reshape(k // 512, 128, 4, n).transpose(0, 1, 3, 2)).astype(ml_dtypes.float8_e4m3fn).view(np.uint8)
    return words, np.ascontiguousarray(byte.astype(np.uint8).reshape(k // 512, 16, n))


def unpack_weight(words, scales):
    g, p, n, _ = words.shape
    vals = np.ascontiguousarray(words).view(ml_dtypes.float8_e4m3fn).astype(np.float64) * np.repeat(np.exp2(scales.astype(np.float64) - 127.0), 8, axis=1)[..., None]
    return vals.transpose(0, 1, 3, 2).reshape(g * 512, n)


E2M1 = np.array([0.0, 0.5, 1.0, 1.5, 2.0, 3.0, 4.0, 6.0, -0.0, -0.5, -1.0, -1.5, -2.0, -3.0, -4.0, -6.0])


def pack_fp4(w):
    k, n = w.shape
    w = f64(np.asarray(w, np.float32).astype(ml_dtypes.bfloat16)).reshape(k // 32, 32, n)
    amax = np.abs(w).max(1)
    mant, ex = np.frexp(amax / 6.0)
    byte = np.clip(np.where(amax > 0, np.where(mant > 0.5, ex, ex - 1) + 127, 1), 1, 254)
    scaled = (w * np.exp2(127.0 - byte)[:, None, :]).reshape(k, n).astype(np.float32)
    c = np.ascontiguousarray(scaled.reshape(k // 512, 128, 4, n).transpose(0, 1, 3, 2)).astype(ml_dtypes.float4_e2m1fn).view(np.uint8) & 0xF
    words = (c[..., 0::2] | (c[..., 1::2] << 4)).reshape(k // 512, 128, 2 * n)
    return np.ascontiguousarray(words), np.ascontiguousarray(byte.astype(np.uint8).reshape(k // 512, 16, n))


def unpack_fp4(words, scales):
    g, _, n = scales.shape
    words = np.ascontiguousarray(words).reshape(g, 128, n, 2)
    nib = np.empty((g, 128, n, 4), np.uint8)
    nib[..., 0::2] = words & 0xF
    nib[..., 1::2] = words >> 4
    vals = E2M1[nib] * np.repeat(np.exp2(scales.astype(np.float64) - 127.0), 8, axis=1)[..., None]
    return vals.transpose(0, 1, 3, 2).reshape(g * 512, n)


def relu(v):
    return np.maximum(v, 0.0)


K, T, S, V, H, N, J = 1024, 2048, 1024, 512, 512, 128, 512


def setup_inputs():
    n = np.random.standard_normal
    s = mx_kscale(K)[:, None]
    u = mx_kscale(H)
    r = mx_kscale(J)[:, None]
    packed_xT = pack_weight(n((K, T)) * s)
    packed_w4 = pack_fp4(n((H, N)) / np.sqrt(H) / u[:, None])
    return {
        "x_words": packed_xT[0],
        "x_scales": packed_xT[1],
        "eT": (n((J, V)) * r).astype(np.float32),
        "w1": (n((K, H)) / np.sqrt(3 * K) / s * u).astype(np.float32),
        "w2": (n((K, H)) / np.sqrt(3 * K) / s * u).astype(np.float32),
        "w3": (n((J, H)) / np.sqrt(3 * J) / r * u).astype(np.float32),
        "w4_words": packed_w4[0],
        "w4_scales": packed_w4[1],
        "offs": striped(np.random.permutation(T)[:S]),
    }


def reference(x_words, x_scales, eT, w1, w2, w3, w4_words, w4_scales, offs):
    xq = unpack_weight(x_words, x_scales)[:, unstriped(offs)]
    h = relu(mxq(f64(w1), 0, "e4m3").T @ xq[:, :V] + mxq(f64(w2), 0, "e4m3").T @ xq[:, V:2 * V] + mxq(f64(w3), 0, "e4m3").T @ mxq(f64(eT), 0, "e4m3"))
    return unpack_fp4(w4_words, w4_scales).T @ mxq(h, 0, "e4m3")

@@ -1,0 +1,168 @@
+from contextlib import ExitStack
+
+import concourse.mybir as mybir
+
+K, T, S, V, H, N, J = 1024, 2048, 1024, 512, 512, 128, 512
+FLOPS = 2 * V * H * (2 * K + J) + 2 * V * H * N
+
+F32 = mybir.dt.float32
+BF16 = mybir.dt.bfloat16
+I32 = mybir.dt.int32
+U32 = mybir.dt.uint32
+U16 = mybir.dt.uint16
+U8 = mybir.dt.uint8
+FP8X4 = mybir.dt.float8_e4m3fn_x4
+FP4X4 = mybir.dt.float4_e2m1fn_x4
+COPY = mybir.ActivationFunctionType.Copy
+RELU = mybir.ActivationFunctionType.Relu
+
+P = 128
+PACK = 4
+K_PASS = P * PACK
+X_PASSES = K // K_PASS
+EDGE_TILE = 128
+EDGE_TILES = V // EDGE_TILE
+QUADRANTS = 4
+SCALAR_COLUMNS = 192
+SCALAR_EDGE_TILES = 2
+
+
+def tile_picked_edgeup_relu_p_kernel(tc, x_words, x_scales, eT, w1, w2, w3, w4_words, w4_scales, offs, out):
+    nc = tc.nc
+
+    with ExitStack() as ctx:
+        keep = ctx.enter_context(tc.tile_pool(name="keep", bufs=1))
+        psum = ctx.enter_context(tc.psum_pool(name="psum", bufs=1))
+        psum2 = ctx.enter_context(tc.psum_pool(name="psum2", bufs=2))
+
+        def load_rows(name, rows):
+            raw = keep.tile([P, PACK, rows.shape[1]], F32, name=name, tag=name, align_bytes=64)
+            nc.sync.dma_start(out=raw[:], in_=rows.rearrange("(p j) w -> p j w", j=PACK))
+            return raw
+
+        def load_node_words(z):
+            words = keep.tile([P, T], U32, name="node_words%d" % z)
+            nc.sync.dma_start(out=words[:].bitcast(I32), in_=x_words[z].rearrange("p n t -> p (n t)").bitcast(I32))
+            return words
+
+        def cast(engine, raw, grouped, c0, c1):
+            src = raw[:, :, c0:c1].rearrange("p j (c i) -> p c j i", i=4)
+            dst = grouped[:, c0:c1, :].rearrange("p (c i) j -> p c j i", i=4)
+            if engine == "scalar":
+                nc.scalar.activation(out=dst, in_=src, func=COPY)
+            else:
+                nc.vector.tensor_copy(out=dst, in_=src)
+
+        def cast_dealt(engine, raw, grouped, c0, c1):
+            src = raw[:, :, c0:c1].rearrange("p j (m t) -> p m j t", t=PACK)
+            dst = grouped[:].rearrange("p (t m) j -> p m j t", t=PACK)[:, c0 // PACK : c1 // PACK, :, :]
+            if engine == "scalar":
+                nc.scalar.activation(out=dst, in_=src, func=COPY)
+            else:
+                nc.vector.tensor_copy(out=dst, in_=src)
+
+        def quantize(name, grouped):
+            width = grouped.shape[1]
+            codes = keep.tile([P, width], U32, name=name + "_codes", align_bytes=64)
+            scales = keep.tile([P, width], U8, name=name + "_scales", align_bytes=64)
+            nc.vector.quantize_mx(out=codes[:].bitcast(FP8X4), scales=scales[:], in_=grouped[:, :, :].rearrange("p w j -> p (w j)"))
+            return codes, scales
+
+        def quantize_weight(name, raw, scalar_columns):
+            grouped = keep.tile([P, H, PACK], BF16, name=name + "_grouped", tag="grouped", align_bytes=64)
+            cast_dealt("scalar", raw, grouped, 0, scalar_columns)
+            if scalar_columns < H:
+                cast_dealt("vector", raw, grouped, scalar_columns, H)
+            return quantize(name, grouped)
+
+        node_scales = keep.tile([P, T], U8, name="node_scales")
+        nc.vector.memset(node_scales[:].bitcast(I32), 0)
+        w4_plane = keep.tile([P, N], U8, name="w4_plane", align_bytes=64)
+        nc.vector.memset(w4_plane[:].bitcast(I32), 0)
+
+        offsets = keep.tile([P, S // 16], U16, name="offsets")
+        node_words = [load_node_words(0)]
+        nc.sync.dma_start(offsets[:], offs)
+        for q in range(QUADRANTS):
+            nc.sync.dma_start(
+                out=node_scales[32 * q : 32 * q + 4 * X_PASSES, :].bitcast(I32),
+                in_=x_scales[:, 4 * q : 4 * q + 4, :].bitcast(I32),
+            )
+        w1a_raw = load_rows("w1a_raw", w1[0:K_PASS, :])
+        node_words.append(load_node_words(1))
+        w2a_raw = load_rows("w2a_raw", w2[0:K_PASS, :])
+        w4_codes = keep.tile([P, 2 * N], U8, name="w4_codes", align_bytes=64)
+        nc.sync.dma_start(out=w4_codes[:].bitcast(I32), in_=w4_words[0].bitcast(I32))
+        for q in range(QUADRANTS):
+            nc.sync.dma_start(
+                out=w4_plane[32 * q : 32 * q + 4, :].bitcast(I32),
+                in_=w4_scales[0, 4 * q : 4 * q + 4, :].bitcast(I32),
+            )
+        w1b_raw = load_rows("w1b_raw", w1[K_PASS:K, :])
+        w2b_raw = load_rows("w2b_raw", w2[K_PASS:K, :])
+        w3_raw = load_rows("w3_raw", w3)
+        e_raw = [load_rows("e_raw%d" % q, eT[:, EDGE_TILE * q : EDGE_TILE * (q + 1)]) for q in range(EDGE_TILES)]
+
+        acc = [psum.tile([P, PACK, EDGE_TILE], F32, name="acc%d" % q) for q in range(EDGE_TILES)]
+
+        def gather_words(z):
+            picked = keep.tile([P, S], U32, name="picked_words%d" % z, align_bytes=64)
+            nc.vector.tensor_copy(picked[:], node_words[z][:].indirect(offsets[:]))
+            return picked
+
+        def add_pass(q, weight, codes, scales, first, last):
+            for t in range(PACK):
+                cols = slice(P * t, P * (t + 1))
+                nc.tensor.matmul_mx(
+                    out=acc[q][:, t, :],
+                    lhsT=weight[0][:, cols].bitcast(FP8X4),
+                    lhsT_scale=weight[1][:, cols],
+                    rhs=codes.bitcast(FP8X4),
+                    rhs_scale=scales,
+                    start=first and t == 0,
+                    stop=last and t == PACK - 1,
+                )
+
+        def node_pass(z, side, picked, weight, start):
+            for q in range(EDGE_TILES):
+                cols = slice(side * V + EDGE_TILE * q, side * V + EDGE_TILE * (q + 1))
+                add_pass(q, weight, picked[:, cols], picked_scales[4 * z : P, cols], start, False)
+
+        picked0 = gather_words(0)
+        picked_scales = keep.tile([P, S], U8, name="picked_scales", align_bytes=64)
+        nc.vector.tensor_copy(picked_scales[:], node_scales[:].indirect(offsets[:]))
+        node_pass(0, 0, picked0, quantize_weight("w1a", w1a_raw, H), True)
+        picked1 = gather_words(1)
+        node_pass(0, 1, picked0, quantize_weight("w2a", w2a_raw, SCALAR_COLUMNS), False)
+        node_pass(1, 0, picked1, quantize_weight("w1b", w1b_raw, SCALAR_COLUMNS), False)
+        node_pass(1, 1, picked1, quantize_weight("w2b", w2b_raw, SCALAR_COLUMNS), False)
+        w3_quantized = quantize_weight("w3", w3_raw, SCALAR_COLUMNS)
+
+        e_first = keep.tile([P, SCALAR_EDGE_TILES, EDGE_TILE, PACK], BF16, name="e_first", tag="w3_raw", align_bytes=64)
+        e_last = keep.tile([P, EDGE_TILES - SCALAR_EDGE_TILES, EDGE_TILE, PACK], BF16, name="e_last", tag="grouped", align_bytes=64)
+        for q in range(EDGE_TILES):
+            grouped = e_first[:, q, :, :] if q < SCALAR_EDGE_TILES else e_last[:, q - SCALAR_EDGE_TILES, :, :]
+            cast("scalar" if q < SCALAR_EDGE_TILES else "vector", e_raw[q], grouped, 0, EDGE_TILE)
+            e_codes, e_scales = quantize("e%d" % q, grouped)
+            add_pass(q, w3_quantized, e_codes[:], e_scales[:], False, True)
+
+        for q in range(EDGE_TILES):
+            grouped = keep.tile([P, EDGE_TILE, PACK], BF16, name="h_grouped%d" % q, align_bytes=64)
+            if q < EDGE_TILES - 1:
+                nc.scalar.activation(out=grouped[:], in_=acc[q][:].rearrange("p t v -> p v t"), func=RELU)
+            else:
+                nc.vector.tensor_scalar_max(grouped[:], acc[q][:].rearrange("p t v -> p v t"), 0.0)
+            h_codes, h_scales = quantize("h%d" % q, grouped)
+            product = psum2.tile([N, EDGE_TILE], F32, name="product")
+            nc.tensor.matmul_mx(
+                out=product[:],
+                lhsT=w4_codes[:].bitcast(FP4X4),
+                lhsT_scale=w4_plane[:],
+                rhs=h_codes[:].bitcast(FP8X4),
+                rhs_scale=h_scales[:],
+                start=True,
+                stop=True,
+            )
+            result = keep.tile([N, EDGE_TILE], F32, name="result%d" % q)
+            nc.scalar.copy(out=result[:], in_=product[:])
+            nc.sync.dma_start(out=out[:, EDGE_TILE * q : EDGE_TILE * (q + 1)], in_=result[:])

@@ -53,8 +53,8 @@ def tile_picked_edgeup_relu_p_kernel(tc, x_words, x_scales, eT, w1, w2, w3, w4_w
             else:
                 nc.vector.tensor_copy(out=dst, in_=src)
 
-        def cast_dealt(engine, raw, grouped, c0, c1):
-            src = raw[:, :, c0:c1].rearrange("p j (m t) -> p m j t", t=PACK)
+        def cast_dealt(engine, raw, grouped, c0, c1, first_column=0):
+            src = raw[:, :, c0 - first_column : c1 - first_column].rearrange("p j (m t) -> p m j t", t=PACK)
             dst = grouped[:].rearrange("p (t m) j -> p m j t", t=PACK)[:, c0 // PACK : c1 // PACK, :, :]
             if engine == "scalar":
                 nc.scalar.activation(out=dst, in_=src, func=COPY)
@@ -69,14 +69,14 @@ def tile_picked_edgeup_relu_p_kernel(tc, x_words, x_scales, eT, w1, w2, w3, w4_w
             return codes, scales
 
         def quantize_weight(name, raw, scalar_columns):
-            grouped = keep.tile([P, H, PACK], BF16, name=name + "_grouped", tag="grouped", align_bytes=64)
+            grouped = keep.tile([P, H, PACK], BF16, name=name + "_grouped", align_bytes=64)
             cast_dealt("scalar", raw, grouped, 0, scalar_columns)
             if scalar_columns < H:
                 cast_dealt("vector", raw, grouped, scalar_columns, H)
             return quantize(name, grouped)
 
         node_scales = keep.tile([P, T], U8, name="node_scales")
-        nc.vector.memset(node_scales[:].bitcast(I32), 0)
+        nc.gpsimd.memset(node_scales[:].bitcast(I32), 0)
         w4_plane = keep.tile([P, N], U8, name="w4_plane", align_bytes=64)
         nc.vector.memset(w4_plane[:].bitcast(I32), 0)
 
@@ -84,13 +84,17 @@ def tile_picked_edgeup_relu_p_kernel(tc, x_words, x_scales, eT, w1, w2, w3, w4_w
         node_words = [load_node_words(0)]
         nc.sync.dma_start(offsets[:], offs)
         for q in range(QUADRANTS):
-            nc.sync.dma_start(
+            nc.gpsimd.dma_start(
                 out=node_scales[32 * q : 32 * q + 4 * X_PASSES, :].bitcast(I32),
                 in_=x_scales[:, 4 * q : 4 * q + 4, :].bitcast(I32),
             )
         w1a_raw = load_rows("w1a_raw", w1[0:K_PASS, :])
         node_words.append(load_node_words(1))
         w2a_raw = load_rows("w2a_raw", w2[0:K_PASS, :])
+        w1b_raw = load_rows("w1b_raw", w1[K_PASS:K, :])
+        w2b_raw = load_rows("w2b_raw", w2[K_PASS:K, :])
+        w3_raw = [load_rows("w3_raw%d" % half, w3[:, half * (H // 2) : (half + 1) * (H // 2)]) for half in range(2)]
+        e_raw = [load_rows("e_raw%d" % q, eT[:, EDGE_TILE * q : EDGE_TILE * (q + 1)]) for q in range(EDGE_TILES)]
         w4_codes = keep.tile([P, 2 * N], U8, name="w4_codes", align_bytes=64)
         nc.sync.dma_start(out=w4_codes[:].bitcast(I32), in_=w4_words[0].bitcast(I32))
         for q in range(QUADRANTS):
@@ -98,10 +102,6 @@ def tile_picked_edgeup_relu_p_kernel(tc, x_words, x_scales, eT, w1, w2, w3, w4_w
                 out=w4_plane[32 * q : 32 * q + 4, :].bitcast(I32),
                 in_=w4_scales[0, 4 * q : 4 * q + 4, :].bitcast(I32),
             )
-        w1b_raw = load_rows("w1b_raw", w1[K_PASS:K, :])
-        w2b_raw = load_rows("w2b_raw", w2[K_PASS:K, :])
-        w3_raw = load_rows("w3_raw", w3)
-        e_raw = [load_rows("e_raw%d" % q, eT[:, EDGE_TILE * q : EDGE_TILE * (q + 1)]) for q in range(EDGE_TILES)]
 
         acc = [psum.tile([P, PACK, EDGE_TILE], F32, name="acc%d" % q) for q in range(EDGE_TILES)]
 
@@ -133,13 +133,23 @@ def tile_picked_edgeup_relu_p_kernel(tc, x_words, x_scales, eT, w1, w2, w3, w4_w
         nc.vector.tensor_copy(picked_scales[:], node_scales[:].indirect(offsets[:]))
         node_pass(0, 0, picked0, quantize_weight("w1a", w1a_raw, H), True)
         picked1 = gather_words(1)
-        node_pass(0, 1, picked0, quantize_weight("w2a", w2a_raw, SCALAR_COLUMNS), False)
-        node_pass(1, 0, picked1, quantize_weight("w1b", w1b_raw, SCALAR_COLUMNS), False)
+        node_pass(0, 1, picked0, quantize_weight("w2a", w2a_raw, 384), False)
+        node_pass(1, 0, picked1, quantize_weight("w1b", w1b_raw, 256), False)
         node_pass(1, 1, picked1, quantize_weight("w2b", w2b_raw, SCALAR_COLUMNS), False)
-        w3_quantized = quantize_weight("w3", w3_raw, SCALAR_COLUMNS)
+        w3_grouped = keep.tile([P, H, PACK], BF16, name="w3_grouped", align_bytes=64)
+        w3_codes = keep.tile([P, H], U32, name="w3_codes", align_bytes=64)
+        w3_scales = keep.tile([P, H], U8, name="w3_scales", align_bytes=64)
+        for half in range(2):
+            c0 = half * (H // 2)
+            cast_dealt("scalar", w3_raw[half], w3_grouped, c0, c0 + SCALAR_COLUMNS // 2, c0)
+            cast_dealt("vector", w3_raw[half], w3_grouped, c0 + SCALAR_COLUMNS // 2, c0 + H // 2, c0)
+            for t in range(PACK):
+                cols = slice(P * t + half * (P // 2), P * t + (half + 1) * (P // 2))
+                nc.vector.quantize_mx(out=w3_codes[:, cols].bitcast(FP8X4), scales=w3_scales[:, cols], in_=w3_grouped[:, cols, :].rearrange("p w j -> p (w j)"))
+        w3_quantized = (w3_codes, w3_scales)
 
-        e_first = keep.tile([P, SCALAR_EDGE_TILES, EDGE_TILE, PACK], BF16, name="e_first", tag="w3_raw", align_bytes=64)
-        e_last = keep.tile([P, EDGE_TILES - SCALAR_EDGE_TILES, EDGE_TILE, PACK], BF16, name="e_last", tag="grouped", align_bytes=64)
+        e_first = keep.tile([P, SCALAR_EDGE_TILES, EDGE_TILE, PACK], BF16, name="e_first", align_bytes=64)
+        e_last = keep.tile([P, EDGE_TILES - SCALAR_EDGE_TILES, EDGE_TILE, PACK], BF16, name="e_last", align_bytes=64)
         for q in range(EDGE_TILES):
             grouped = e_first[:, q, :, :] if q < SCALAR_EDGE_TILES else e_last[:, q - SCALAR_EDGE_TILES, :, :]
             cast("scalar" if q < SCALAR_EDGE_TILES else "vector", e_raw[q], grouped, 0, EDGE_TILE)

@@ -61,11 +61,13 @@ def tile_picked_edgeup_relu_p_kernel(tc, x_words, x_scales, eT, w1, w2, w3, w4_w
             else:
                 nc.vector.tensor_copy(out=dst, in_=src)
 
-        def quantize(name, grouped):
+        def quantize(name, grouped, pieces=1):
             width = grouped.shape[1]
             codes = keep.tile([P, width], U32, name=name + "_codes", align_bytes=64)
             scales = keep.tile([P, width], U8, name=name + "_scales", align_bytes=64)
-            nc.vector.quantize_mx(out=codes[:].bitcast(FP8X4), scales=scales[:], in_=grouped[:, :, :].rearrange("p w j -> p (w j)"))
+            for piece in range(pieces):
+                cols = slice(piece * width // pieces, (piece + 1) * width // pieces)
+                nc.vector.quantize_mx(out=codes[:, cols].bitcast(FP8X4), scales=scales[:, cols], in_=grouped[:, cols, :].rearrange("p w j -> p (w j)"))
             return codes, scales
 
         def quantize_weight(name, raw, scalar_columns):
@@ -81,15 +83,14 @@ def tile_picked_edgeup_relu_p_kernel(tc, x_words, x_scales, eT, w1, w2, w3, w4_w
         nc.vector.memset(w4_plane[:].bitcast(I32), 0)
 
         offsets = keep.tile([P, S // 16], U16, name="offsets")
-        node_words = [load_node_words(0)]
+        w1a_raw = load_rows("w1a_raw", w1[0:K_PASS, :])
         nc.sync.dma_start(offsets[:], offs)
         for q in range(QUADRANTS):
-            nc.gpsimd.dma_start(
+            nc.sync.dma_start(
                 out=node_scales[32 * q : 32 * q + 4 * X_PASSES, :].bitcast(I32),
                 in_=x_scales[:, 4 * q : 4 * q + 4, :].bitcast(I32),
             )
-        w1a_raw = load_rows("w1a_raw", w1[0:K_PASS, :])
-        node_words.append(load_node_words(1))
+        node_words = [load_node_words(z) for z in range(X_PASSES)]
         w2a_raw = load_rows("w2a_raw", w2[0:K_PASS, :])
         w1b_raw = load_rows("w1b_raw", w1[K_PASS:K, :])
         w2b_raw = load_rows("w2b_raw", w2[K_PASS:K, :])
@@ -128,9 +129,9 @@ def tile_picked_edgeup_relu_p_kernel(tc, x_words, x_scales, eT, w1, w2, w3, w4_w
                 cols = slice(side * V + EDGE_TILE * q, side * V + EDGE_TILE * (q + 1))
                 add_pass(q, weight, picked[:, cols], picked_scales[4 * z : P, cols], start, False)
 
-        picked0 = gather_words(0)
         picked_scales = keep.tile([P, S], U8, name="picked_scales", align_bytes=64)
         nc.vector.tensor_copy(picked_scales[:], node_scales[:].indirect(offsets[:]))
+        picked0 = gather_words(0)
         node_pass(0, 0, picked0, quantize_weight("w1a", w1a_raw, H), True)
         picked1 = gather_words(1)
         node_pass(0, 1, picked0, quantize_weight("w2a", w2a_raw, 384), False)
@@ -152,8 +153,10 @@ def tile_picked_edgeup_relu_p_kernel(tc, x_words, x_scales, eT, w1, w2, w3, w4_w
         e_last = keep.tile([P, EDGE_TILES - SCALAR_EDGE_TILES, EDGE_TILE, PACK], BF16, name="e_last", align_bytes=64)
         for q in range(EDGE_TILES):
             grouped = e_first[:, q, :, :] if q < SCALAR_EDGE_TILES else e_last[:, q - SCALAR_EDGE_TILES, :, :]
-            cast("scalar" if q < SCALAR_EDGE_TILES else "vector", e_raw[q], grouped, 0, EDGE_TILE)
-            e_codes, e_scales = quantize("e%d" % q, grouped)
+            pieces = 2 if q == EDGE_TILES - 1 else 1
+            for piece in range(pieces):
+                cast("scalar" if q < SCALAR_EDGE_TILES else "vector", e_raw[q], grouped, piece * EDGE_TILE // pieces, (piece + 1) * EDGE_TILE // pieces)
+            e_codes, e_scales = quantize("e%d" % q, grouped, pieces)
             add_pass(q, w3_quantized, e_codes[:], e_scales[:], False, True)
 
         for q in range(EDGE_TILES):
@@ -161,8 +164,10 @@ def tile_picked_edgeup_relu_p_kernel(tc, x_words, x_scales, eT, w1, w2, w3, w4_w
             if q < EDGE_TILES - 1:
                 nc.scalar.activation(out=grouped[:], in_=acc[q][:].rearrange("p t v -> p v t"), func=RELU)
             else:
-                nc.vector.tensor_scalar_max(grouped[:], acc[q][:].rearrange("p t v -> p v t"), 0.0)
-            h_codes, h_scales = quantize("h%d" % q, grouped)
+                for piece in range(2):
+                    cols = slice(piece * EDGE_TILE // 2, (piece + 1) * EDGE_TILE // 2)
+                    nc.vector.tensor_scalar_max(grouped[:, cols, :], acc[q][:, :, cols].rearrange("p t v -> p v t"), 0.0)
+            h_codes, h_scales = quantize("h%d" % q, grouped, 2 if q == EDGE_TILES - 1 else 1)
             product = psum2.tile([N, EDGE_TILE], F32, name="product")
             nc.tensor.matmul_mx(
                 out=product[:],

@@ -78,7 +78,7 @@ def tile_picked_edgeup_relu_p_kernel(tc, x_words, x_scales, eT, w1, w2, w3, w4_w
             return quantize(name, grouped)
 
         node_scales = keep.tile([P, T], U8, name="node_scales")
-        nc.gpsimd.memset(node_scales[:].bitcast(I32), 0)
+        nc.vector.memset(node_scales[:].bitcast(I32), 0)
         w4_plane = keep.tile([P, N], U8, name="w4_plane", align_bytes=64)
         nc.vector.memset(w4_plane[:].bitcast(I32), 0)
 
@@ -94,8 +94,8 @@ def tile_picked_edgeup_relu_p_kernel(tc, x_words, x_scales, eT, w1, w2, w3, w4_w
         w2a_raw = load_rows("w2a_raw", w2[0:K_PASS, :])
         w1b_raw = load_rows("w1b_raw", w1[K_PASS:K, :])
         w2b_raw = load_rows("w2b_raw", w2[K_PASS:K, :])
-        w3_raw = [load_rows("w3_raw%d" % half, w3[:, half * (H // 2) : (half + 1) * (H // 2)]) for half in range(2)]
-        e_raw = [load_rows("e_raw%d" % q, eT[:, EDGE_TILE * q : EDGE_TILE * (q + 1)]) for q in range(EDGE_TILES)]
+        w3_raw = load_rows("w3_raw", w3)
+        e_raw = [load_rows("e_raw%d" % half, eT[:, half * (V // 2) : (half + 1) * (V // 2)]) for half in range(2)]
         w4_codes = keep.tile([P, 2 * N], U8, name="w4_codes", align_bytes=64)
         nc.sync.dma_start(out=w4_codes[:].bitcast(I32), in_=w4_words[0].bitcast(I32))
         for q in range(QUADRANTS):
@@ -137,35 +137,24 @@ def tile_picked_edgeup_relu_p_kernel(tc, x_words, x_scales, eT, w1, w2, w3, w4_w
         node_pass(0, 1, picked0, quantize_weight("w2a", w2a_raw, 384), False)
         node_pass(1, 0, picked1, quantize_weight("w1b", w1b_raw, 256), False)
         node_pass(1, 1, picked1, quantize_weight("w2b", w2b_raw, SCALAR_COLUMNS), False)
-        w3_grouped = keep.tile([P, H, PACK], BF16, name="w3_grouped", align_bytes=64)
-        w3_codes = keep.tile([P, H], U32, name="w3_codes", align_bytes=64)
-        w3_scales = keep.tile([P, H], U8, name="w3_scales", align_bytes=64)
-        for half in range(2):
-            c0 = half * (H // 2)
-            cast_dealt("scalar", w3_raw[half], w3_grouped, c0, c0 + SCALAR_COLUMNS // 2, c0)
-            cast_dealt("vector", w3_raw[half], w3_grouped, c0 + SCALAR_COLUMNS // 2, c0 + H // 2, c0)
-            for t in range(PACK):
-                cols = slice(P * t + half * (P // 2), P * t + (half + 1) * (P // 2))
-                nc.vector.quantize_mx(out=w3_codes[:, cols].bitcast(FP8X4), scales=w3_scales[:, cols], in_=w3_grouped[:, cols, :].rearrange("p w j -> p (w j)"))
-        w3_quantized = (w3_codes, w3_scales)
+        w3_quantized = quantize_weight("w3", w3_raw, SCALAR_COLUMNS)
 
-        e_first = keep.tile([P, SCALAR_EDGE_TILES, EDGE_TILE, PACK], BF16, name="e_first", align_bytes=64)
-        e_last = keep.tile([P, EDGE_TILES - SCALAR_EDGE_TILES, EDGE_TILE, PACK], BF16, name="e_last", align_bytes=64)
+        e_grouped = [keep.tile([P, 2, EDGE_TILE, PACK], BF16, name="e_grouped%d" % half, tag="e_grouped%d" % half, align_bytes=64) for half in range(2)]
         for q in range(EDGE_TILES):
-            grouped = e_first[:, q, :, :] if q < SCALAR_EDGE_TILES else e_last[:, q - SCALAR_EDGE_TILES, :, :]
-            pieces = 2 if q == EDGE_TILES - 1 else 1
-            for piece in range(pieces):
-                cast("scalar" if q < SCALAR_EDGE_TILES else "vector", e_raw[q], grouped, piece * EDGE_TILE // pieces, (piece + 1) * EDGE_TILE // pieces)
-            e_codes, e_scales = quantize("e%d" % q, grouped, pieces)
+            half, tile_in_half = divmod(q, 2)
+            grouped = e_grouped[half][:, tile_in_half, :, :]
+            cast("scalar" if q in (0, 3) else "vector", e_raw[half][:, :, EDGE_TILE * tile_in_half : EDGE_TILE * (tile_in_half + 1)], grouped, 0, EDGE_TILE)
+            e_codes, e_scales = quantize("e%d" % q, grouped)
             add_pass(q, w3_quantized, e_codes[:], e_scales[:], False, True)
 
         for q in range(EDGE_TILES):
-            grouped = keep.tile([P, EDGE_TILE, PACK], BF16, name="h_grouped%d" % q, align_bytes=64)
-            if q < EDGE_TILES - 1:
+            grouped = keep.tile([P, EDGE_TILE, PACK], BF16, name="h_grouped%d" % q, tag=("e_raw1", "e_grouped1", "h_grouped2", "h_grouped3")[q], align_bytes=64)
+            if q % 2 == 0:
                 nc.scalar.activation(out=grouped[:], in_=acc[q][:].rearrange("p t v -> p v t"), func=RELU)
             else:
-                for piece in range(2):
-                    cols = slice(piece * EDGE_TILE // 2, (piece + 1) * EDGE_TILE // 2)
+                pieces = 2 if q == EDGE_TILES - 1 else 1
+                for piece in range(pieces):
+                    cols = slice(piece * EDGE_TILE // pieces, (piece + 1) * EDGE_TILE // pieces)
                     nc.vector.tensor_scalar_max(grouped[:, cols, :], acc[q][:, :, cols].rearrange("p t v -> p v t"), 0.0)
             h_codes, h_scales = quantize("h%d" % q, grouped, 2 if q == EDGE_TILES - 1 else 1)
             product = psum2.tile([N, EDGE_TILE], F32, name="product")

@@ -33,7 +33,7 @@ def tile_picked_edgeup_relu_p_kernel(tc, x_words, x_scales, eT, w1, w2, w3, w4_w
     with ExitStack() as ctx:
         keep = ctx.enter_context(tc.tile_pool(name="keep", bufs=1))
         psum = ctx.enter_context(tc.psum_pool(name="psum", bufs=1))
-        psum2 = ctx.enter_context(tc.psum_pool(name="psum2", bufs=2))
+        psum2 = ctx.enter_context(tc.psum_pool(name="psum2", bufs=4))
 
         def load_rows(name, rows):
             raw = keep.tile([P, PACK, rows.shape[1]], F32, name=name, tag=name, align_bytes=64)
@@ -148,15 +148,12 @@ def tile_picked_edgeup_relu_p_kernel(tc, x_words, x_scales, eT, w1, w2, w3, w4_w
             add_pass(q, w3_quantized, e_codes[:], e_scales[:], False, True)
 
         for q in range(EDGE_TILES):
-            grouped = keep.tile([P, EDGE_TILE, PACK], BF16, name="h_grouped%d" % q, tag=("e_raw1", "e_grouped1", "h_grouped2", "h_grouped3")[q], align_bytes=64)
-            if q % 2 == 0:
+            grouped = keep.tile([P, EDGE_TILE, PACK], BF16, name="h_grouped%d" % q, tag=("e_raw1", "h_grouped1", "e_grouped1", "h_grouped3")[q], align_bytes=64)
+            if q != 2:
                 nc.scalar.activation(out=grouped[:], in_=acc[q][:].rearrange("p t v -> p v t"), func=RELU)
             else:
-                pieces = 2 if q == EDGE_TILES - 1 else 1
-                for piece in range(pieces):
-                    cols = slice(piece * EDGE_TILE // pieces, (piece + 1) * EDGE_TILE // pieces)
-                    nc.vector.tensor_scalar_max(grouped[:, cols, :], acc[q][:, :, cols].rearrange("p t v -> p v t"), 0.0)
-            h_codes, h_scales = quantize("h%d" % q, grouped, 2 if q == EDGE_TILES - 1 else 1)
+                nc.vector.tensor_scalar_max(grouped[:], acc[q][:].rearrange("p t v -> p v t"), 0.0)
+            h_codes, h_scales = quantize("h%d" % q, grouped)
             product = psum2.tile([N, EDGE_TILE], F32, name="product")
             nc.tensor.matmul_mx(
                 out=product[:],
@@ -168,5 +165,8 @@ def tile_picked_edgeup_relu_p_kernel(tc, x_words, x_scales, eT, w1, w2, w3, w4_w
                 stop=True,
             )
             result = keep.tile([N, EDGE_TILE], F32, name="result%d" % q)
-            nc.scalar.copy(out=result[:], in_=product[:])
+            if q < EDGE_TILES - 1:
+                nc.scalar.copy(out=result[:], in_=product[:])
+            else:
+                nc.vector.tensor_copy(out=result[:], in_=product[:])
             nc.sync.dma_start(out=out[:, EDGE_TILE * q : EDGE_TILE * (q + 1)], in_=result[:])

@@ -23,8 +23,6 @@ X_PASSES = K // K_PASS
 EDGE_TILE = 128
 EDGE_TILES = V // EDGE_TILE
 QUADRANTS = 4
-SCALAR_COLUMNS = 192
-SCALAR_EDGE_TILES = 2
 
 
 def tile_picked_edgeup_relu_p_kernel(tc, x_words, x_scales, eT, w1, w2, w3, w4_words, w4_scales, offs, out):
@@ -33,10 +31,15 @@ def tile_picked_edgeup_relu_p_kernel(tc, x_words, x_scales, eT, w1, w2, w3, w4_w
     with ExitStack() as ctx:
         keep = ctx.enter_context(tc.tile_pool(name="keep", bufs=1))
         psum = ctx.enter_context(tc.psum_pool(name="psum", bufs=1))
-        psum2 = ctx.enter_context(tc.psum_pool(name="psum2", bufs=4))
+
+        def copy_on(engine, dst, src):
+            if engine == "scalar":
+                nc.scalar.activation(out=dst, in_=src, func=COPY)
+            else:
+                nc.vector.tensor_copy(out=dst, in_=src)
 
         def load_rows(name, rows):
-            raw = keep.tile([P, PACK, rows.shape[1]], F32, name=name, tag=name, align_bytes=64)
+            raw = keep.tile([P, PACK, rows.shape[1]], F32, name=name, align_bytes=64)
             nc.sync.dma_start(out=raw[:], in_=rows.rearrange("(p j) w -> p j w", j=PACK))
             return raw
 
@@ -45,21 +48,13 @@ def tile_picked_edgeup_relu_p_kernel(tc, x_words, x_scales, eT, w1, w2, w3, w4_w
             nc.sync.dma_start(out=words[:].bitcast(I32), in_=x_words[z].rearrange("p n t -> p (n t)").bitcast(I32))
             return words
 
-        def cast(engine, raw, grouped, c0, c1):
-            src = raw[:, :, c0:c1].rearrange("p j (c i) -> p c j i", i=4)
-            dst = grouped[:, c0:c1, :].rearrange("p (c i) j -> p c j i", i=4)
-            if engine == "scalar":
-                nc.scalar.activation(out=dst, in_=src, func=COPY)
-            else:
-                nc.vector.tensor_copy(out=dst, in_=src)
+        def cast(engine, raw, grouped):
+            copy_on(engine, grouped.rearrange("p (c i) j -> p c j i", i=4), raw.rearrange("p j (c i) -> p c j i", i=4))
 
-        def cast_dealt(engine, raw, grouped, c0, c1, first_column=0):
-            src = raw[:, :, c0 - first_column : c1 - first_column].rearrange("p j (m t) -> p m j t", t=PACK)
+        def cast_dealt(engine, raw, grouped, c0, c1):
+            src = raw[:, :, c0:c1].rearrange("p j (m t) -> p m j t", t=PACK)
             dst = grouped[:].rearrange("p (t m) j -> p m j t", t=PACK)[:, c0 // PACK : c1 // PACK, :, :]
-            if engine == "scalar":
-                nc.scalar.activation(out=dst, in_=src, func=COPY)
-            else:
-                nc.vector.tensor_copy(out=dst, in_=src)
+            copy_on(engine, dst, src)
 
         def quantize(name, grouped, pieces=1):
             width = grouped.shape[1]
@@ -70,39 +65,15 @@ def tile_picked_edgeup_relu_p_kernel(tc, x_words, x_scales, eT, w1, w2, w3, w4_w
                 nc.vector.quantize_mx(out=codes[:, cols].bitcast(FP8X4), scales=scales[:, cols], in_=grouped[:, cols, :].rearrange("p w j -> p (w j)"))
             return codes, scales
 
-        def quantize_weight(name, raw, scalar_columns):
+        def cast_weight(name, raw, scalar_columns):
             grouped = keep.tile([P, H, PACK], BF16, name=name + "_grouped", align_bytes=64)
             cast_dealt("scalar", raw, grouped, 0, scalar_columns)
             if scalar_columns < H:
                 cast_dealt("vector", raw, grouped, scalar_columns, H)
-            return quantize(name, grouped)
+            return grouped
 
-        node_scales = keep.tile([P, T], U8, name="node_scales")
-        nc.vector.memset(node_scales[:].bitcast(I32), 0)
-        w4_plane = keep.tile([P, N], U8, name="w4_plane", align_bytes=64)
-        nc.vector.memset(w4_plane[:].bitcast(I32), 0)
-
-        offsets = keep.tile([P, S // 16], U16, name="offsets")
-        w1a_raw = load_rows("w1a_raw", w1[0:K_PASS, :])
-        nc.sync.dma_start(offsets[:], offs)
-        for q in range(QUADRANTS):
-            nc.sync.dma_start(
-                out=node_scales[32 * q : 32 * q + 4 * X_PASSES, :].bitcast(I32),
-                in_=x_scales[:, 4 * q : 4 * q + 4, :].bitcast(I32),
-            )
-        node_words = [load_node_words(z) for z in range(X_PASSES)]
-        w2a_raw = load_rows("w2a_raw", w2[0:K_PASS, :])
-        w1b_raw = load_rows("w1b_raw", w1[K_PASS:K, :])
-        w2b_raw = load_rows("w2b_raw", w2[K_PASS:K, :])
-        w3_raw = load_rows("w3_raw", w3)
-        e_raw = [load_rows("e_raw%d" % half, eT[:, half * (V // 2) : (half + 1) * (V // 2)]) for half in range(2)]
-        w4_codes = keep.tile([P, 2 * N], U8, name="w4_codes", align_bytes=64)
-        nc.sync.dma_start(out=w4_codes[:].bitcast(I32), in_=w4_words[0].bitcast(I32))
-        for q in range(QUADRANTS):
-            nc.sync.dma_start(
-                out=w4_plane[32 * q : 32 * q + 4, :].bitcast(I32),
-                in_=w4_scales[0, 4 * q : 4 * q + 4, :].bitcast(I32),
-            )
+        def quantize_weight(name, raw, scalar_columns, pieces=1):
+            return quantize(name, cast_weight(name, raw, scalar_columns), pieces)
 
         acc = [psum.tile([P, PACK, EDGE_TILE], F32, name="acc%d" % q) for q in range(EDGE_TILES)]
 
@@ -129,32 +100,27 @@ def tile_picked_edgeup_relu_p_kernel(tc, x_words, x_scales, eT, w1, w2, w3, w4_w
                 cols = slice(side * V + EDGE_TILE * q, side * V + EDGE_TILE * (q + 1))
                 add_pass(q, weight, picked[:, cols], picked_scales[4 * z : P, cols], start, False)
 
-        picked_scales = keep.tile([P, S], U8, name="picked_scales", align_bytes=64)
-        nc.vector.tensor_copy(picked_scales[:], node_scales[:].indirect(offsets[:]))
-        picked0 = gather_words(0)
-        node_pass(0, 0, picked0, quantize_weight("w1a", w1a_raw, H), True)
-        picked1 = gather_words(1)
-        node_pass(0, 1, picked0, quantize_weight("w2a", w2a_raw, 384), False)
-        node_pass(1, 0, picked1, quantize_weight("w1b", w1b_raw, 256), False)
-        node_pass(1, 1, picked1, quantize_weight("w2b", w2b_raw, SCALAR_COLUMNS), False)
-        w3_quantized = quantize_weight("w3", w3_raw, SCALAR_COLUMNS)
+        def cast_edges(q, engine):
+            raw, first = e_raw[q]
+            grouped = keep.tile([P, EDGE_TILE, PACK], BF16, name="e_grouped%d" % q, align_bytes=64)
+            cast(engine, raw[:, :, first : first + EDGE_TILE], grouped[:])
+            return grouped
 
-        e_grouped = [keep.tile([P, 2, EDGE_TILE, PACK], BF16, name="e_grouped%d" % half, tag="e_grouped%d" % half, align_bytes=64) for half in range(2)]
-        for q in range(EDGE_TILES):
-            half, tile_in_half = divmod(q, 2)
-            grouped = e_grouped[half][:, tile_in_half, :, :]
-            cast("scalar" if q in (0, 3) else "vector", e_raw[half][:, :, EDGE_TILE * tile_in_half : EDGE_TILE * (tile_in_half + 1)], grouped, 0, EDGE_TILE)
+        def edge_pass(q, grouped):
             e_codes, e_scales = quantize("e%d" % q, grouped)
             add_pass(q, w3_quantized, e_codes[:], e_scales[:], False, True)
 
-        for q in range(EDGE_TILES):
-            grouped = keep.tile([P, EDGE_TILE, PACK], BF16, name="h_grouped%d" % q, tag=("e_raw1", "h_grouped1", "e_grouped1", "h_grouped3")[q], align_bytes=64)
-            if q != 2:
+        def relu(q, engine):
+            grouped = keep.tile([P, EDGE_TILE, PACK], BF16, name="h_grouped%d" % q, align_bytes=64)
+            if engine == "scalar":
                 nc.scalar.activation(out=grouped[:], in_=acc[q][:].rearrange("p t v -> p v t"), func=RELU)
             else:
                 nc.vector.tensor_scalar_max(grouped[:], acc[q][:].rearrange("p t v -> p v t"), 0.0)
+            return grouped
+
+        def second_layer(q, grouped):
             h_codes, h_scales = quantize("h%d" % q, grouped)
-            product = psum2.tile([N, EDGE_TILE], F32, name="product")
+            product = psum.tile([N, EDGE_TILE], F32, name="product%d" % q)
             nc.tensor.matmul_mx(
                 out=product[:],
                 lhsT=w4_codes[:].bitcast(FP4X4),
@@ -164,9 +130,71 @@ def tile_picked_edgeup_relu_p_kernel(tc, x_words, x_scales, eT, w1, w2, w3, w4_w
                 start=True,
                 stop=True,
             )
+            return product
+
+        def store(q, product, engine):
             result = keep.tile([N, EDGE_TILE], F32, name="result%d" % q)
-            if q < EDGE_TILES - 1:
-                nc.scalar.copy(out=result[:], in_=product[:])
-            else:
-                nc.vector.tensor_copy(out=result[:], in_=product[:])
+            copy_on(engine, result[:], product[:])
             nc.sync.dma_start(out=out[:, EDGE_TILE * q : EDGE_TILE * (q + 1)], in_=result[:])
+
+        node_scales = keep.tile([P, T], U8, name="node_scales")
+        nc.vector.memset(node_scales[:].bitcast(I32), 0)
+        w4_plane = keep.tile([P, N], U8, name="w4_plane", align_bytes=64)
+        nc.vector.memset(w4_plane[:].bitcast(I32), 0)
+
+        offsets = keep.tile([P, S // 16], U16, name="offsets")
+        w1a_raw = load_rows("w1a_raw", w1[0:K_PASS, :])
+        nc.sync.dma_start(offsets[:], offs)
+        for q in range(QUADRANTS):
+            nc.sync.dma_start(
+                out=node_scales[32 * q : 32 * q + 4 * X_PASSES, :].bitcast(I32),
+                in_=x_scales[:, 4 * q : 4 * q + 4, :].bitcast(I32),
+            )
+        node_words = [load_node_words(0)]
+        w2a_raw = load_rows("w2a_raw", w2[0:K_PASS, :])
+        node_words.append(load_node_words(1))
+        w1b_raw = load_rows("w1b_raw", w1[K_PASS:K, :])
+        w2b_raw = load_rows("w2b_raw", w2[K_PASS:K, :])
+        w3_raw = load_rows("w3_raw", w3)
+        e_raw = []
+        for first_tile, tiles in ((0, 1), (1, 1), (2, 1), (3, 1)):
+            raw = load_rows("e_raw%d" % first_tile, eT[:, first_tile * EDGE_TILE : (first_tile + tiles) * EDGE_TILE])
+            e_raw.extend((raw, i * EDGE_TILE) for i in range(tiles))
+        w4_codes = keep.tile([P, 2 * N], U8, name="w4_codes", align_bytes=64)
+        nc.sync.dma_start(out=w4_codes[:].bitcast(I32), in_=w4_words[0].bitcast(I32))
+        for q in range(QUADRANTS):
+            nc.sync.dma_start(
+                out=w4_plane[32 * q : 32 * q + 4, :].bitcast(I32),
+                in_=w4_scales[0, 4 * q : 4 * q + 4, :].bitcast(I32),
+            )
+
+        picked_scales = keep.tile([P, S], U8, name="picked_scales", align_bytes=64)
+        nc.vector.tensor_copy(picked_scales[:], node_scales[:].indirect(offsets[:]))
+        picked0 = gather_words(0)
+        node_pass(0, 0, picked0, quantize_weight("w1a", w1a_raw, 512), True)
+        node_pass(0, 1, picked0, quantize_weight("w2a", w2a_raw, 320), False)
+        picked1 = gather_words(1)
+        node_pass(1, 0, picked1, quantize_weight("w1b", w1b_raw, 256), False)
+        node_pass(1, 1, picked1, quantize_weight("w2b", w2b_raw, 192), False)
+        w3_quantized = quantize_weight("w3", w3_raw, 176, 1)
+
+        e0 = cast_edges(0, "scalar")
+        edge_pass(0, e0)
+        e1 = cast_edges(1, "scalar")
+        e2 = cast_edges(2, "vector")
+        edge_pass(1, e1)
+        e3 = cast_edges(3, "vector")
+        edge_pass(2, e2)
+        edge_pass(3, e3)
+        h0 = relu(0, "scalar")
+        p0 = second_layer(0, h0)
+        h1 = relu(1, "scalar")
+        h2 = relu(2, "vector")
+        p1 = second_layer(1, h1)
+        h3 = relu(3, "scalar")
+        p2 = second_layer(2, h2)
+        p3 = second_layer(3, h3)
+        store(0, p0, "scalar")
+        store(1, p1, "scalar")
+        store(2, p2, "scalar")
+        store(3, p3, "vector")

@@ -118,11 +118,10 @@ def tile_picked_edgeup_relu_p_kernel(tc, x_words, x_scales, eT, w1, w2, w3, w4_w
                 nc.vector.tensor_scalar_max(grouped[:], acc[q][:].rearrange("p t v -> p v t"), 0.0)
             return grouped
 
-        def second_layer(q, grouped):
+        def second_layer(q, grouped, product):
             h_codes, h_scales = quantize("h%d" % q, grouped)
-            product = psum.tile([N, EDGE_TILE], F32, name="product%d" % q)
             nc.tensor.matmul_mx(
-                out=product[:],
+                out=product,
                 lhsT=w4_codes[:].bitcast(FP4X4),
                 lhsT_scale=w4_plane[:],
                 rhs=h_codes[:].bitcast(FP8X4),
@@ -130,12 +129,12 @@ def tile_picked_edgeup_relu_p_kernel(tc, x_words, x_scales, eT, w1, w2, w3, w4_w
                 start=True,
                 stop=True,
             )
-            return product
 
-        def store(q, product, engine):
-            result = keep.tile([N, EDGE_TILE], F32, name="result%d" % q)
+        def store(first_tile, product, engine):
+            width = product.shape[1]
+            result = keep.tile([N, width], F32, name="result%d" % first_tile)
             copy_on(engine, result[:], product[:])
-            nc.sync.dma_start(out=out[:, EDGE_TILE * q : EDGE_TILE * (q + 1)], in_=result[:])
+            nc.sync.dma_start(out=out[:, EDGE_TILE * first_tile : EDGE_TILE * first_tile + width], in_=result[:])
 
         node_scales = keep.tile([P, T], U8, name="node_scales")
         nc.vector.memset(node_scales[:].bitcast(I32), 0)
@@ -143,16 +142,16 @@ def tile_picked_edgeup_relu_p_kernel(tc, x_words, x_scales, eT, w1, w2, w3, w4_w
         nc.vector.memset(w4_plane[:].bitcast(I32), 0)
 
         offsets = keep.tile([P, S // 16], U16, name="offsets")
-        w1a_raw = load_rows("w1a_raw", w1[0:K_PASS, :])
+        node_words = [load_node_words(0)]
         nc.sync.dma_start(offsets[:], offs)
         for q in range(QUADRANTS):
             nc.sync.dma_start(
                 out=node_scales[32 * q : 32 * q + 4 * X_PASSES, :].bitcast(I32),
                 in_=x_scales[:, 4 * q : 4 * q + 4, :].bitcast(I32),
             )
-        node_words = [load_node_words(0)]
-        w2a_raw = load_rows("w2a_raw", w2[0:K_PASS, :])
+        w1a_raw = load_rows("w1a_raw", w1[0:K_PASS, :])
         node_words.append(load_node_words(1))
+        w2a_raw = load_rows("w2a_raw", w2[0:K_PASS, :])
         w1b_raw = load_rows("w1b_raw", w1[K_PASS:K, :])
         w2b_raw = load_rows("w2b_raw", w2[K_PASS:K, :])
         w3_raw = load_rows("w3_raw", w3)
@@ -168,33 +167,35 @@ def tile_picked_edgeup_relu_p_kernel(tc, x_words, x_scales, eT, w1, w2, w3, w4_w
                 in_=w4_scales[0, 4 * q : 4 * q + 4, :].bitcast(I32),
             )
 
+        picked0 = gather_words(0)
         picked_scales = keep.tile([P, S], U8, name="picked_scales", align_bytes=64)
         nc.vector.tensor_copy(picked_scales[:], node_scales[:].indirect(offsets[:]))
-        picked0 = gather_words(0)
         node_pass(0, 0, picked0, quantize_weight("w1a", w1a_raw, 512), True)
-        node_pass(0, 1, picked0, quantize_weight("w2a", w2a_raw, 320), False)
         picked1 = gather_words(1)
-        node_pass(1, 0, picked1, quantize_weight("w1b", w1b_raw, 256), False)
-        node_pass(1, 1, picked1, quantize_weight("w2b", w2b_raw, 192), False)
-        w3_quantized = quantize_weight("w3", w3_raw, 176, 1)
+        node_pass(0, 1, picked0, quantize_weight("w2a", w2a_raw, 320), False)
+        node_pass(1, 0, picked1, quantize_weight("w1b", w1b_raw, 320), False)
+        node_pass(1, 1, picked1, quantize_weight("w2b", w2b_raw, 256), False)
+        w3_quantized = quantize_weight("w3", w3_raw, 176)
 
         e0 = cast_edges(0, "scalar")
-        edge_pass(0, e0)
         e1 = cast_edges(1, "scalar")
-        e2 = cast_edges(2, "vector")
+        edge_pass(0, e0)
+        e2 = cast_edges(2, "scalar")
         edge_pass(1, e1)
         e3 = cast_edges(3, "vector")
         edge_pass(2, e2)
         edge_pass(3, e3)
+        p01 = psum.tile([N, 2 * EDGE_TILE], F32, name="product01")
+        p2 = psum.tile([N, EDGE_TILE], F32, name="product2")
+        p3 = psum.tile([N, EDGE_TILE], F32, name="product3")
         h0 = relu(0, "scalar")
-        p0 = second_layer(0, h0)
+        second_layer(0, h0, p01[:, 0:EDGE_TILE])
         h1 = relu(1, "scalar")
         h2 = relu(2, "vector")
-        p1 = second_layer(1, h1)
+        second_layer(1, h1, p01[:, EDGE_TILE : 2 * EDGE_TILE])
         h3 = relu(3, "scalar")
-        p2 = second_layer(2, h2)
-        p3 = second_layer(3, h3)
-        store(0, p0, "scalar")
-        store(1, p1, "scalar")
+        second_layer(2, h2, p2[:])
+        second_layer(3, h3, p3[:])
+        store(0, p01, "scalar")
         store(2, p2, "scalar")
         store(3, p3, "vector")

@@ -142,13 +142,13 @@ def tile_picked_edgeup_relu_p_kernel(tc, x_words, x_scales, eT, w1, w2, w3, w4_w
         nc.vector.memset(w4_plane[:].bitcast(I32), 0)
 
         offsets = keep.tile([P, S // 16], U16, name="offsets")
-        node_words = [load_node_words(0)]
+        scale_rows = keep.tile([P, T], U8, name="scale_rows")
+        for q in (2, 3, 0, 1):
+            rows = slice(32 * q, 32 * q + 4 * X_PASSES)
+            nc.sync.dma_start(out=scale_rows[rows, :].bitcast(I32), in_=x_scales[:, 4 * q : 4 * q + 4, :].bitcast(I32))
+            nc.vector.tensor_copy(out=node_scales[rows, :].bitcast(I32), in_=scale_rows[rows, :].bitcast(I32))
         nc.sync.dma_start(offsets[:], offs)
-        for q in range(QUADRANTS):
-            nc.sync.dma_start(
-                out=node_scales[32 * q : 32 * q + 4 * X_PASSES, :].bitcast(I32),
-                in_=x_scales[:, 4 * q : 4 * q + 4, :].bitcast(I32),
-            )
+        node_words = [load_node_words(0)]
         w1a_raw = load_rows("w1a_raw", w1[0:K_PASS, :])
         node_words.append(load_node_words(1))
         w2a_raw = load_rows("w2a_raw", w2[0:K_PASS, :])
@@ -167,9 +167,9 @@ def tile_picked_edgeup_relu_p_kernel(tc, x_words, x_scales, eT, w1, w2, w3, w4_w
                 in_=w4_scales[0, 4 * q : 4 * q + 4, :].bitcast(I32),
             )
 
-        picked0 = gather_words(0)
         picked_scales = keep.tile([P, S], U8, name="picked_scales", align_bytes=64)
         nc.vector.tensor_copy(picked_scales[:], node_scales[:].indirect(offsets[:]))
+        picked0 = gather_words(0)
         node_pass(0, 0, picked0, quantize_weight("w1a", w1a_raw, 512), True)
         picked1 = gather_words(1)
         node_pass(0, 1, picked0, quantize_weight("w2a", w2a_raw, 320), False)

@@ -100,10 +100,13 @@ def tile_picked_edgeup_relu_p_kernel(tc, x_words, x_scales, eT, w1, w2, w3, w4_w
                 cols = slice(side * V + EDGE_TILE * q, side * V + EDGE_TILE * (q + 1))
                 add_pass(q, weight, picked[:, cols], picked_scales[4 * z : P, cols], start, False)
 
-        def cast_edges(q, engine):
+        def cast_edges(q, vector_columns):
             raw, first = e_raw[q]
-            grouped = keep.tile([P, EDGE_TILE, PACK], BF16, name="e_grouped%d" % q, align_bytes=64)
-            cast(engine, raw[:, :, first : first + EDGE_TILE], grouped[:])
+            grouped = keep.tile([P, EDGE_TILE, PACK], BF16, name="e_grouped%d" % q, tag="e_grouped%d" % (0 if q == 2 else q), align_bytes=64)
+            if vector_columns > 0:
+                cast("vector", raw[:, :, first : first + vector_columns], grouped[:, 0:vector_columns, :])
+            if vector_columns < EDGE_TILE:
+                cast("scalar", raw[:, :, first + vector_columns : first + EDGE_TILE], grouped[:, vector_columns:EDGE_TILE, :])
             return grouped
 
         def edge_pass(q, grouped):
@@ -156,7 +159,7 @@ def tile_picked_edgeup_relu_p_kernel(tc, x_words, x_scales, eT, w1, w2, w3, w4_w
         w2b_raw = load_rows("w2b_raw", w2[K_PASS:K, :])
         w3_raw = load_rows("w3_raw", w3)
         e_raw = []
-        for first_tile, tiles in ((0, 1), (1, 1), (2, 1), (3, 1)):
+        for first_tile, tiles in ((0, 2), (2, 1), (3, 1)):
             raw = load_rows("e_raw%d" % first_tile, eT[:, first_tile * EDGE_TILE : (first_tile + tiles) * EDGE_TILE])
             e_raw.extend((raw, i * EDGE_TILE) for i in range(tiles))
         w4_codes = keep.tile([P, 2 * N], U8, name="w4_codes", align_bytes=64)
@@ -177,12 +180,12 @@ def tile_picked_edgeup_relu_p_kernel(tc, x_words, x_scales, eT, w1, w2, w3, w4_w
         node_pass(1, 1, picked1, quantize_weight("w2b", w2b_raw, 256), False)
         w3_quantized = quantize_weight("w3", w3_raw, 176)
 
-        e0 = cast_edges(0, "scalar")
-        e1 = cast_edges(1, "scalar")
+        e0 = cast_edges(0, 0)
+        e1 = cast_edges(1, 0)
         edge_pass(0, e0)
-        e2 = cast_edges(2, "scalar")
+        e2 = cast_edges(2, 128)
         edge_pass(1, e1)
-        e3 = cast_edges(3, "vector")
+        e3 = cast_edges(3, 80)
         edge_pass(2, e2)
         edge_pass(3, e3)
         p01 = psum.tile([N, 2 * EDGE_TILE], F32, name="product01")

@@ -38,13 +38,13 @@ def tile_picked_edgeup_relu_p_kernel(tc, x_words, x_scales, eT, w1, w2, w3, w4_w
             else:
                 nc.vector.tensor_copy(out=dst, in_=src)
 
-        def load_rows(name, rows):
-            raw = keep.tile([P, PACK, rows.shape[1]], F32, name=name, align_bytes=64)
+        def load_rows(name, rows, tag):
+            raw = keep.tile([P, PACK, rows.shape[1]], F32, name=name, tag=tag, align_bytes=64)
             nc.sync.dma_start(out=raw[:], in_=rows.rearrange("(p j) w -> p j w", j=PACK))
             return raw
 
         def load_node_words(z):
-            words = keep.tile([P, T], U32, name="node_words%d" % z)
+            words = keep.tile([P, T], U32, name="node_words%d" % z, align_bytes=64)
             nc.sync.dma_start(out=words[:].bitcast(I32), in_=x_words[z].rearrange("p n t -> p (n t)").bitcast(I32))
             return words
 
@@ -66,7 +66,7 @@ def tile_picked_edgeup_relu_p_kernel(tc, x_words, x_scales, eT, w1, w2, w3, w4_w
             return codes, scales
 
         def cast_weight(name, raw, scalar_columns):
-            grouped = keep.tile([P, H, PACK], BF16, name=name + "_grouped", align_bytes=64)
+            grouped = keep.tile([P, H, PACK], BF16, name=name + "_grouped", tag=name + "_grouped", align_bytes=64)
             cast_dealt("scalar", raw, grouped, 0, scalar_columns)
             if scalar_columns < H:
                 cast_dealt("vector", raw, grouped, scalar_columns, H)
@@ -139,45 +139,55 @@ def tile_picked_edgeup_relu_p_kernel(tc, x_words, x_scales, eT, w1, w2, w3, w4_w
             copy_on(engine, result[:], product[:])
             nc.sync.dma_start(out=out[:, EDGE_TILE * first_tile : EDGE_TILE * first_tile + width], in_=result[:])
 
-        node_scales = keep.tile([P, T], U8, name="node_scales")
-        nc.vector.memset(node_scales[:].bitcast(I32), 0)
-        w4_plane = keep.tile([P, N], U8, name="w4_plane", align_bytes=64)
-        nc.vector.memset(w4_plane[:].bitcast(I32), 0)
+        node_scales = keep.tile([P, T], U8, name="node_scales", align_bytes=64)
+        nc.vector.memset(node_scales[32:64, :].bitcast(I32), 0)
+        nc.vector.memset(node_scales[64:P, :].bitcast(I32), 0)
+        picked_scales = keep.tile([P, S], U8, name="picked_scales", align_bytes=64)
+        nc.vector.memset(picked_scales[:].bitcast(I32), 0)
 
         offsets = keep.tile([P, S // 16], U16, name="offsets")
-        scale_rows = keep.tile([P, T], U8, name="scale_rows")
-        for q in (2, 3, 0, 1):
-            rows = slice(32 * q, 32 * q + 4 * X_PASSES)
-            nc.sync.dma_start(out=scale_rows[rows, :].bitcast(I32), in_=x_scales[:, 4 * q : 4 * q + 4, :].bitcast(I32))
-            nc.vector.tensor_copy(out=node_scales[rows, :].bitcast(I32), in_=scale_rows[rows, :].bitcast(I32))
+        nc.sync.dma_start(out=node_scales[0:32, :].bitcast(I32), in_=x_scales.rearrange("z q n -> (z q) n").bitcast(I32))
         nc.sync.dma_start(offsets[:], offs)
         node_words = [load_node_words(0)]
-        w1a_raw = load_rows("w1a_raw", w1[0:K_PASS, :])
+        w1a_raw = load_rows("w1a_raw", w1[0:K_PASS, :], "w1a_raw")
         node_words.append(load_node_words(1))
-        w2a_raw = load_rows("w2a_raw", w2[0:K_PASS, :])
-        w1b_raw = load_rows("w1b_raw", w1[K_PASS:K, :])
-        w2b_raw = load_rows("w2b_raw", w2[K_PASS:K, :])
-        w3_raw = load_rows("w3_raw", w3)
-        e_raw = []
-        for first_tile, tiles in ((0, 2), (2, 1), (3, 1)):
-            raw = load_rows("e_raw%d" % first_tile, eT[:, first_tile * EDGE_TILE : (first_tile + tiles) * EDGE_TILE])
-            e_raw.extend((raw, i * EDGE_TILE) for i in range(tiles))
-        w4_codes = keep.tile([P, 2 * N], U8, name="w4_codes", align_bytes=64)
-        nc.sync.dma_start(out=w4_codes[:].bitcast(I32), in_=w4_words[0].bitcast(I32))
+
+        picked_rows = keep.tile([P, S], U8, name="picked_rows", align_bytes=64)
+        nc.vector.tensor_copy(picked_rows[:], node_scales[:].indirect(offsets[:]))
+
+        def move_scale_rows(z):
+            for r in range(4):
+                nc.sync.dma_start(
+                    out=picked_scales[4 * z + r : P : 32, :].bitcast(I32),
+                    in_=picked_rows[16 * z + r : 16 * (z + 1) : 4, :].bitcast(I32),
+                )
+
+        move_scale_rows(0)
+        w2a_raw = load_rows("w2a_raw", w2[0:K_PASS, :], "node_scales")
+        move_scale_rows(1)
+        picked0 = gather_words(0)
+        w1b_raw = load_rows("w1b_raw", w1[K_PASS:K, :], "node_words0")
+        node_pass(0, 0, picked0, quantize_weight("w1a", w1a_raw, 512), True)
+        w2b_raw = load_rows("w2b_raw", w2[K_PASS:K, :], "w1a_raw")
+        picked1 = gather_words(1)
+        w3_raw = load_rows("w3_raw", w3, "node_words1")
+        node_pass(0, 1, picked0, quantize_weight("w2a", w2a_raw, 320), False)
+        e_first = load_rows("e_raw0", eT[:, 0 : 2 * EDGE_TILE], "node_scales")
+        node_pass(1, 0, picked1, quantize_weight("w1b", w1b_raw, 320), False)
+        e_last = keep.tile([P, 2, PACK, EDGE_TILE], F32, name="e_last", tag="node_words0", align_bytes=64)
+        for i in range(2):
+            nc.sync.dma_start(out=e_last[:, i], in_=eT[:, (2 + i) * EDGE_TILE : (3 + i) * EDGE_TILE].rearrange("(p j) w -> p j w", j=PACK))
+        e_raw = [(e_first, 0), (e_first, EDGE_TILE), (e_last[:, 0], 0), (e_last[:, 1], 0)]
+        w4_plane = keep.tile([P, N], U8, name="w4_plane", tag="w1b_grouped", align_bytes=64)
+        nc.vector.memset(w4_plane[:].bitcast(I32), 0)
         for q in range(QUADRANTS):
             nc.sync.dma_start(
                 out=w4_plane[32 * q : 32 * q + 4, :].bitcast(I32),
                 in_=w4_scales[0, 4 * q : 4 * q + 4, :].bitcast(I32),
             )
-
-        picked_scales = keep.tile([P, S], U8, name="picked_scales", align_bytes=64)
-        nc.vector.tensor_copy(picked_scales[:], node_scales[:].indirect(offsets[:]))
-        picked0 = gather_words(0)
-        node_pass(0, 0, picked0, quantize_weight("w1a", w1a_raw, 512), True)
-        picked1 = gather_words(1)
-        node_pass(0, 1, picked0, quantize_weight("w2a", w2a_raw, 320), False)
-        node_pass(1, 0, picked1, quantize_weight("w1b", w1b_raw, 320), False)
         node_pass(1, 1, picked1, quantize_weight("w2b", w2b_raw, 256), False)
+        w4_codes = keep.tile([P, 2 * N], U8, name="w4_codes", tag="w1a_raw", align_bytes=64)
+        nc.sync.dma_start(out=w4_codes[:].bitcast(I32), in_=w4_words[0].bitcast(I32))
         w3_quantized = quantize_weight("w3", w3_raw, 176)
 
         e0 = cast_edges(0, 0)

@@ -56,9 +56,9 @@ def tile_picked_edgeup_relu_p_kernel(tc, x_words, x_scales, eT, w1, w2, w3, w4_w
             dst = grouped[:].rearrange("p (t m) j -> p m j t", t=PACK)[:, c0 // PACK : c1 // PACK, :, :]
             copy_on(engine, dst, src)
 
-        def quantize(name, grouped, pieces=1):
+        def quantize(name, grouped, pieces=1, tag=None):
             width = grouped.shape[1]
-            codes = keep.tile([P, width], U32, name=name + "_codes", align_bytes=64)
+            codes = keep.tile([P, width], U32, name=name + "_codes", tag=tag or name + "_codes", align_bytes=64)
             scales = keep.tile([P, width], U8, name=name + "_scales", align_bytes=64)
             for piece in range(pieces):
                 cols = slice(piece * width // pieces, (piece + 1) * width // pieces)
@@ -82,9 +82,9 @@ def tile_picked_edgeup_relu_p_kernel(tc, x_words, x_scales, eT, w1, w2, w3, w4_w
             nc.vector.tensor_copy(picked[:], node_words[z][:].indirect(offsets[:]))
             return picked
 
-        def add_pass(q, weight, codes, scales, first, last):
-            for t in range(PACK):
-                cols = slice(P * t, P * (t + 1))
+        def add_pass(q, weight, codes, scales, first, last, products=range(PACK)):
+            for t in products:
+                cols = slice(P * (t - products[0]), P * (t - products[0] + 1))
                 nc.tensor.matmul_mx(
                     out=acc[q][:, t, :],
                     lhsT=weight[0][:, cols].bitcast(FP8X4),
@@ -95,10 +95,10 @@ def tile_picked_edgeup_relu_p_kernel(tc, x_words, x_scales, eT, w1, w2, w3, w4_w
                     stop=last and t == PACK - 1,
                 )
 
-        def node_pass(z, side, picked, weight, start):
+        def node_pass(z, side, picked, weight, start, products=range(PACK)):
             for q in range(EDGE_TILES):
                 cols = slice(side * V + EDGE_TILE * q, side * V + EDGE_TILE * (q + 1))
-                add_pass(q, weight, picked[:, cols], picked_scales[4 * z : P, cols], start, False)
+                add_pass(q, weight, picked[:, cols], picked_scales[4 * z : P, cols], start, False, products)
 
         def cast_edges(q, vector_columns):
             raw, first = e_raw[q]
@@ -140,13 +140,13 @@ def tile_picked_edgeup_relu_p_kernel(tc, x_words, x_scales, eT, w1, w2, w3, w4_w
             nc.sync.dma_start(out=out[:, EDGE_TILE * first_tile : EDGE_TILE * first_tile + width], in_=result[:])
 
         node_scales = keep.tile([P, T], U8, name="node_scales", align_bytes=64)
-        nc.vector.memset(node_scales[32:64, :].bitcast(I32), 0)
-        nc.vector.memset(node_scales[64:P, :].bitcast(I32), 0)
+        nc.vector.memset(node_scales[0:64, :].bitcast(I32), 0)
+        nc.vector.memset(node_scales[96:P, :].bitcast(I32), 0)
         picked_scales = keep.tile([P, S], U8, name="picked_scales", align_bytes=64)
         nc.vector.memset(picked_scales[:].bitcast(I32), 0)
 
         offsets = keep.tile([P, S // 16], U16, name="offsets")
-        nc.sync.dma_start(out=node_scales[0:32, :].bitcast(I32), in_=x_scales.rearrange("z q n -> (z q) n").bitcast(I32))
+        nc.sync.dma_start(out=node_scales[64:96, :].bitcast(I32), in_=x_scales.rearrange("z q n -> (z q) n").bitcast(I32))
         nc.sync.dma_start(offsets[:], offs)
         node_words = [load_node_words(0)]
         w1a_raw = load_rows("w1a_raw", w1[0:K_PASS, :], "w1a_raw")
@@ -155,16 +155,17 @@ def tile_picked_edgeup_relu_p_kernel(tc, x_words, x_scales, eT, w1, w2, w3, w4_w
         picked_rows = keep.tile([P, S], U8, name="picked_rows", align_bytes=64)
         nc.vector.tensor_copy(picked_rows[:], node_scales[:].indirect(offsets[:]))
 
-        def move_scale_rows(z):
-            for r in range(4):
-                nc.sync.dma_start(
-                    out=picked_scales[4 * z + r : P : 32, :].bitcast(I32),
-                    in_=picked_rows[16 * z + r : 16 * (z + 1) : 4, :].bitcast(I32),
-                )
+        def move_scale_rows(first, last):
+            for r in range(first, last):
+                for z in range(X_PASSES):
+                    nc.sync.dma_start(
+                        out=picked_scales[4 * z + r : P : 32, :].bitcast(I32),
+                        in_=picked_rows[64 + 16 * z + r : 64 + 16 * (z + 1) : 4, :].bitcast(I32),
+                    )
 
-        move_scale_rows(0)
+        move_scale_rows(0, 2)
         w2a_raw = load_rows("w2a_raw", w2[0:K_PASS, :], "node_scales")
-        move_scale_rows(1)
+        move_scale_rows(2, 4)
         picked0 = gather_words(0)
         w1b_raw = load_rows("w1b_raw", w1[K_PASS:K, :], "node_words0")
         node_pass(0, 0, picked0, quantize_weight("w1a", w1a_raw, 512), True)
@@ -185,10 +186,13 @@ def tile_picked_edgeup_relu_p_kernel(tc, x_words, x_scales, eT, w1, w2, w3, w4_w
                 out=w4_plane[32 * q : 32 * q + 4, :].bitcast(I32),
                 in_=w4_scales[0, 4 * q : 4 * q + 4, :].bitcast(I32),
             )
-        node_pass(1, 1, picked1, quantize_weight("w2b", w2b_raw, 256), False)
+        w2b_grouped = cast_weight("w2b", w2b_raw, 256)
+        node_pass(1, 1, picked1, quantize("w2b_low", w2b_grouped[:, 0 : 2 * P, :]), False, range(0, 2))
         w4_codes = keep.tile([P, 2 * N], U8, name="w4_codes", tag="w1a_raw", align_bytes=64)
         nc.sync.dma_start(out=w4_codes[:].bitcast(I32), in_=w4_words[0].bitcast(I32))
-        w3_quantized = quantize_weight("w3", w3_raw, 176)
+        w3_grouped = cast_weight("w3", w3_raw, 176)
+        node_pass(1, 1, picked1, quantize("w2b_high", w2b_grouped[:, 2 * P : 4 * P, :], tag="node_words1"), False, range(2, 4))
+        w3_quantized = quantize("w3", w3_grouped)
 
         e0 = cast_edges(0, 0)
         e1 = cast_edges(1, 0)

@@ -43,11 +43,6 @@ def tile_picked_edgeup_relu_p_kernel(tc, x_words, x_scales, eT, w1, w2, w3, w4_w
             nc.sync.dma_start(out=raw[:], in_=rows.rearrange("(p j) w -> p j w", j=PACK))
             return raw
 
-        def load_node_words(z):
-            words = keep.tile([P, T], U32, name="node_words%d" % z, align_bytes=64)
-            nc.sync.dma_start(out=words[:].bitcast(I32), in_=x_words[z].rearrange("p n t -> p (n t)").bitcast(I32))
-            return words
-
         def cast(engine, raw, grouped):
             copy_on(engine, grouped.rearrange("p (c i) j -> p c j i", i=4), raw.rearrange("p j (c i) -> p c j i", i=4))
 
@@ -79,7 +74,7 @@ def tile_picked_edgeup_relu_p_kernel(tc, x_words, x_scales, eT, w1, w2, w3, w4_w
 
         def gather_words(z):
             picked = keep.tile([P, S], U32, name="picked_words%d" % z, align_bytes=64)
-            nc.vector.tensor_copy(picked[:], node_words[z][:].indirect(offsets[:]))
+            nc.vector.tensor_copy(picked[:], node_words[:, z, :].indirect(offsets[:]))
             return picked
 
         def add_pass(q, weight, codes, scales, first, last, products=range(PACK)):
@@ -98,11 +93,11 @@ def tile_picked_edgeup_relu_p_kernel(tc, x_words, x_scales, eT, w1, w2, w3, w4_w
         def node_pass(z, side, picked, weight, start, products=range(PACK)):
             for q in range(EDGE_TILES):
                 cols = slice(side * V + EDGE_TILE * q, side * V + EDGE_TILE * (q + 1))
-                add_pass(q, weight, picked[:, cols], picked_scales[4 * z : P, cols], start, False, products)
+                add_pass(q, weight, picked[:, cols], picked_scales[z][4 * z : P, cols], start, False, products)
 
         def cast_edges(q, vector_columns):
             raw, first = e_raw[q]
-            grouped = keep.tile([P, EDGE_TILE, PACK], BF16, name="e_grouped%d" % q, tag="e_grouped%d" % (0 if q == 2 else q), align_bytes=64)
+            grouped = keep.tile([P, EDGE_TILE, PACK], BF16, name="e_grouped%d" % q, align_bytes=64)
             if vector_columns > 0:
                 cast("vector", raw[:, :, first : first + vector_columns], grouped[:, 0:vector_columns, :])
             if vector_columns < EDGE_TILE:
@@ -133,73 +128,74 @@ def tile_picked_edgeup_relu_p_kernel(tc, x_words, x_scales, eT, w1, w2, w3, w4_w
                 stop=True,
             )
 
-        def store(first_tile, product, engine):
-            width = product.shape[1]
-            result = keep.tile([N, width], F32, name="result%d" % first_tile)
-            copy_on(engine, result[:], product[:])
-            nc.sync.dma_start(out=out[:, EDGE_TILE * first_tile : EDGE_TILE * first_tile + width], in_=result[:])
+        def store(first_tile, products):
+            result = keep.tile([N, 2 * EDGE_TILE], F32, name="result%d" % first_tile)
+            column = 0
+            for product, engine in products:
+                copy_on(engine, result[:, column : column + product.shape[1]], product[:])
+                column = column + product.shape[1]
+            nc.sync.dma_start(out=out[:, EDGE_TILE * first_tile : EDGE_TILE * (first_tile + 2)], in_=result[:])
 
         node_scales = keep.tile([P, T], U8, name="node_scales", align_bytes=64)
         nc.vector.memset(node_scales[0:64, :].bitcast(I32), 0)
         nc.vector.memset(node_scales[96:P, :].bitcast(I32), 0)
-        picked_scales = keep.tile([P, S], U8, name="picked_scales", align_bytes=64)
-        nc.vector.memset(picked_scales[:].bitcast(I32), 0)
+        picked_scales = []
+        for z in range(X_PASSES):
+            plane = keep.tile([P, S], U8, name="picked_scales%d" % z, align_bytes=64)
+            nc.vector.memset(plane[:].bitcast(I32), 0)
+            picked_scales.append(plane)
 
         offsets = keep.tile([P, S // 16], U16, name="offsets")
         nc.sync.dma_start(out=node_scales[64:96, :].bitcast(I32), in_=x_scales.rearrange("z q n -> (z q) n").bitcast(I32))
         nc.sync.dma_start(offsets[:], offs)
-        node_words = [load_node_words(0)]
-        w1a_raw = load_rows("w1a_raw", w1[0:K_PASS, :], "w1a_raw")
-        node_words.append(load_node_words(1))
+        node_words = keep.tile([P, X_PASSES, T], U32, name="node_words", tag="node_words", align_bytes=64)
+        nc.sync.dma_start(out=node_words[:].bitcast(I32), in_=x_words.rearrange("z p n t -> p z (n t)").bitcast(I32))
+        w1_raw = keep.tile([P, X_PASSES, PACK, H], F32, name="w1_raw", tag="w1_raw", align_bytes=64)
+        nc.sync.dma_start(out=w1_raw[:], in_=w1.rearrange("(z p j) w -> p z j w", z=X_PASSES, j=PACK))
 
         picked_rows = keep.tile([P, S], U8, name="picked_rows", align_bytes=64)
         nc.vector.tensor_copy(picked_rows[:], node_scales[:].indirect(offsets[:]))
 
-        def move_scale_rows(first, last):
-            for r in range(first, last):
-                for z in range(X_PASSES):
-                    nc.sync.dma_start(
-                        out=picked_scales[4 * z + r : P : 32, :].bitcast(I32),
-                        in_=picked_rows[64 + 16 * z + r : 64 + 16 * (z + 1) : 4, :].bitcast(I32),
-                    )
+        def move_scale_rows(moves):
+            for z, r in moves:
+                nc.sync.dma_start(
+                    out=picked_scales[z][4 * z + r : P : 32, :].bitcast(I32),
+                    in_=picked_rows[64 + 16 * z + r : 64 + 16 * (z + 1) : 4, :].bitcast(I32),
+                )
 
-        move_scale_rows(0, 2)
+        move_scale_rows([(0, 0), (1, 0), (0, 1), (1, 1), (0, 2), (0, 3)])
         w2a_raw = load_rows("w2a_raw", w2[0:K_PASS, :], "node_scales")
-        move_scale_rows(2, 4)
+        move_scale_rows([(1, 2), (1, 3)])
         picked0 = gather_words(0)
-        w1b_raw = load_rows("w1b_raw", w1[K_PASS:K, :], "node_words0")
-        node_pass(0, 0, picked0, quantize_weight("w1a", w1a_raw, 512), True)
-        w2b_raw = load_rows("w2b_raw", w2[K_PASS:K, :], "w1a_raw")
         picked1 = gather_words(1)
-        w3_raw = load_rows("w3_raw", w3, "node_words1")
-        node_pass(0, 1, picked0, quantize_weight("w2a", w2a_raw, 320), False)
-        e_first = load_rows("e_raw0", eT[:, 0 : 2 * EDGE_TILE], "node_scales")
-        node_pass(1, 0, picked1, quantize_weight("w1b", w1b_raw, 320), False)
-        e_last = keep.tile([P, 2, PACK, EDGE_TILE], F32, name="e_last", tag="node_words0", align_bytes=64)
-        for i in range(2):
-            nc.sync.dma_start(out=e_last[:, i], in_=eT[:, (2 + i) * EDGE_TILE : (3 + i) * EDGE_TILE].rearrange("(p j) w -> p j w", j=PACK))
-        e_raw = [(e_first, 0), (e_first, EDGE_TILE), (e_last[:, 0], 0), (e_last[:, 1], 0)]
-        w4_plane = keep.tile([P, N], U8, name="w4_plane", tag="w1b_grouped", align_bytes=64)
+        w2b_raw = load_rows("w2b_raw", w2[K_PASS:K, :], "node_words")
+        node_pass(0, 0, picked0, quantize_weight("w1a", w1_raw[:, 0], 256), True)
+        w1b_grouped = cast_weight("w1b", w1_raw[:, 1], 256)
+        w3_raw = load_rows("w3_raw", w3, "w1a_grouped")
+        node_pass(1, 0, picked1, quantize("w1b", w1b_grouped), False)
+        e_first = load_rows("e_raw0", eT[:, 0 : 2 * EDGE_TILE], "w1b_grouped")
+        w2a_grouped = cast_weight("w2a", w2a_raw, 320)
+        e_last = load_rows("e_raw1", eT[:, 2 * EDGE_TILE : V], "node_scales")
+        e_raw = [(e_first, 0), (e_first, EDGE_TILE), (e_last, 0), (e_last, EDGE_TILE)]
+        node_pass(0, 1, picked0, quantize("w2a", w2a_grouped), False)
+        w4_codes = keep.tile([P, 2 * N], U8, name="w4_codes", tag="w2a_grouped", align_bytes=64)
+        nc.sync.dma_start(out=w4_codes[:].bitcast(I32), in_=w4_words[0].bitcast(I32))
+        node_pass(1, 1, picked1, quantize_weight("w2b", w2b_raw, 336), False)
+        w4_plane = keep.tile([P, N], U8, name="w4_plane", tag="node_words", align_bytes=64)
         nc.vector.memset(w4_plane[:].bitcast(I32), 0)
         for q in range(QUADRANTS):
             nc.sync.dma_start(
                 out=w4_plane[32 * q : 32 * q + 4, :].bitcast(I32),
                 in_=w4_scales[0, 4 * q : 4 * q + 4, :].bitcast(I32),
             )
-        w2b_grouped = cast_weight("w2b", w2b_raw, 256)
-        node_pass(1, 1, picked1, quantize("w2b_low", w2b_grouped[:, 0 : 2 * P, :]), False, range(0, 2))
-        w4_codes = keep.tile([P, 2 * N], U8, name="w4_codes", tag="w1a_raw", align_bytes=64)
-        nc.sync.dma_start(out=w4_codes[:].bitcast(I32), in_=w4_words[0].bitcast(I32))
-        w3_grouped = cast_weight("w3", w3_raw, 176)
-        node_pass(1, 1, picked1, quantize("w2b_high", w2b_grouped[:, 2 * P : 4 * P, :], tag="node_words1"), False, range(2, 4))
-        w3_quantized = quantize("w3", w3_grouped)
+        w3_quantized = quantize_weight("w3", w3_raw, 192)
 
         e0 = cast_edges(0, 0)
         e1 = cast_edges(1, 0)
         edge_pass(0, e0)
         e2 = cast_edges(2, 128)
         edge_pass(1, e1)
-        e3 = cast_edges(3, 80)
+        e3 = cast_edges(3, 0)
         edge_pass(2, e2)
         edge_pass(3, e3)
         p01 = psum.tile([N, 2 * EDGE_TILE], F32, name="product01")
@@ -213,6 +209,5 @@ def tile_picked_edgeup_relu_p_kernel(tc, x_words, x_scales, eT, w1, w2, w3, w4_w
         h3 = relu(3, "scalar")
         second_layer(2, h2, p2[:])
         second_layer(3, h3, p3[:])
-        store(0, p01, "scalar")
-        store(2, p2, "scalar")
-        store(3, p3, "vector")
+        store(0, [(p01, "scalar")])
+        store(2, [(p2, "scalar"), (p3, "vector")])

@@ -22,7 +22,9 @@ K_PASS = P * PACK
 X_PASSES = K // K_PASS
 EDGE_TILE = 128
 EDGE_TILES = V // EDGE_TILE
-QUADRANTS = 4
+QUADRANT = 32
+QUADRANTS = P // QUADRANT
+SCALE_ROWS = 4
 
 
 def tile_picked_edgeup_relu_p_kernel(tc, x_words, x_scales, eT, w1, w2, w3, w4_words, w4_scales, offs, out):
@@ -32,54 +34,60 @@ def tile_picked_edgeup_relu_p_kernel(tc, x_words, x_scales, eT, w1, w2, w3, w4_w
         keep = ctx.enter_context(tc.tile_pool(name="keep", bufs=1))
         psum = ctx.enter_context(tc.psum_pool(name="psum", bufs=1))
 
+        def sbuf(name, shape, dtype, reuses=None):
+            return keep.tile(shape, dtype, name=name, tag=reuses or name, align_bytes=64)
+
         def copy_on(engine, dst, src):
             if engine == "scalar":
                 nc.scalar.activation(out=dst, in_=src, func=COPY)
             else:
                 nc.vector.tensor_copy(out=dst, in_=src)
 
-        def load_rows(name, rows, tag):
-            raw = keep.tile([P, PACK, rows.shape[1]], F32, name=name, tag=tag, align_bytes=64)
+        def load_rows(name, rows, reuses=None):
+            raw = sbuf(name, [P, PACK, rows.shape[1]], F32, reuses)
             nc.sync.dma_start(out=raw[:], in_=rows.rearrange("(p j) w -> p j w", j=PACK))
             return raw
 
-        def cast(engine, raw, grouped):
-            copy_on(engine, grouped.rearrange("p (c i) j -> p c j i", i=4), raw.rearrange("p j (c i) -> p c j i", i=4))
+        def load_words(z):
+            words = sbuf("node_words%d" % z, [P, T], U32)
+            nc.sync.dma_start(out=words[:].bitcast(I32), in_=x_words[z].rearrange("p n t -> p (n t)").bitcast(I32))
+            return words
 
-        def cast_dealt(engine, raw, grouped, c0, c1):
-            src = raw[:, :, c0:c1].rearrange("p j (m t) -> p m j t", t=PACK)
-            dst = grouped[:].rearrange("p (t m) j -> p m j t", t=PACK)[:, c0 // PACK : c1 // PACK, :, :]
-            copy_on(engine, dst, src)
-
-        def quantize(name, grouped, pieces=1, tag=None):
-            width = grouped.shape[1]
-            codes = keep.tile([P, width], U32, name=name + "_codes", tag=tag or name + "_codes", align_bytes=64)
-            scales = keep.tile([P, width], U8, name=name + "_scales", align_bytes=64)
-            for piece in range(pieces):
-                cols = slice(piece * width // pieces, (piece + 1) * width // pieces)
-                nc.vector.quantize_mx(out=codes[:, cols].bitcast(FP8X4), scales=scales[:, cols], in_=grouped[:, cols, :].rearrange("p w j -> p (w j)"))
-            return codes, scales
+        def gather_words(z, words, reuses=None):
+            picked = sbuf("picked_words%d" % z, [P, S], U32, reuses)
+            nc.vector.tensor_copy(picked[:], words[:].indirect(offsets[:]))
+            return picked
 
         def cast_weight(name, raw, scalar_columns):
-            grouped = keep.tile([P, H, PACK], BF16, name=name + "_grouped", tag=name + "_grouped", align_bytes=64)
-            cast_dealt("scalar", raw, grouped, 0, scalar_columns)
-            if scalar_columns < H:
-                cast_dealt("vector", raw, grouped, scalar_columns, H)
+            grouped = sbuf(name + "_grouped", [P, H, PACK], BF16)
+            for engine, c0, c1 in (("scalar", 0, scalar_columns), ("vector", scalar_columns, H)):
+                if c1 > c0:
+                    src = raw[:, :, c0:c1].rearrange("p j (m t) -> p m j t", t=PACK)
+                    dst = grouped[:].rearrange("p (t m) j -> p m j t", t=PACK)[:, c0 // PACK : c1 // PACK, :, :]
+                    copy_on(engine, dst, src)
             return grouped
 
-        def quantize_weight(name, raw, scalar_columns, pieces=1):
-            return quantize(name, cast_weight(name, raw, scalar_columns), pieces)
+        def cast_edges(q, vector_columns):
+            raw, first = e_raw[q]
+            grouped = sbuf("e_grouped%d" % q, [P, EDGE_TILE, PACK], BF16)
+            for engine, c0, c1 in (("vector", 0, vector_columns), ("scalar", vector_columns, EDGE_TILE)):
+                if c1 > c0:
+                    src = raw[:, :, first + c0 : first + c1].rearrange("p j (c i) -> p c j i", i=4)
+                    copy_on(engine, grouped[:, c0:c1, :].rearrange("p (c i) j -> p c j i", i=4), src)
+            return grouped
+
+        def quantize(name, grouped):
+            width = grouped.shape[1]
+            codes = sbuf(name + "_codes", [P, width], U32)
+            scales = sbuf(name + "_scales", [P, width], U8)
+            nc.vector.quantize_mx(out=codes[:].bitcast(FP8X4), scales=scales[:], in_=grouped[:].rearrange("p w j -> p (w j)"))
+            return codes, scales
 
         acc = [psum.tile([P, PACK, EDGE_TILE], F32, name="acc%d" % q) for q in range(EDGE_TILES)]
 
-        def gather_words(z):
-            picked = keep.tile([P, S], U32, name="picked_words%d" % z, align_bytes=64)
-            nc.vector.tensor_copy(picked[:], node_words[:, z, :].indirect(offsets[:]))
-            return picked
-
-        def add_pass(q, weight, codes, scales, first, last, products=range(PACK)):
-            for t in products:
-                cols = slice(P * (t - products[0]), P * (t - products[0] + 1))
+        def add_pass(q, weight, codes, scales, first, last):
+            for t in range(PACK):
+                cols = slice(P * t, P * (t + 1))
                 nc.tensor.matmul_mx(
                     out=acc[q][:, t, :],
                     lhsT=weight[0][:, cols].bitcast(FP8X4),
@@ -90,26 +98,17 @@ def tile_picked_edgeup_relu_p_kernel(tc, x_words, x_scales, eT, w1, w2, w3, w4_w
                     stop=last and t == PACK - 1,
                 )
 
-        def node_pass(z, side, picked, weight, start, products=range(PACK)):
+        def node_pass(z, side, picked, weight, first):
             for q in range(EDGE_TILES):
                 cols = slice(side * V + EDGE_TILE * q, side * V + EDGE_TILE * (q + 1))
-                add_pass(q, weight, picked[:, cols], picked_scales[z][4 * z : P, cols], start, False, products)
-
-        def cast_edges(q, vector_columns):
-            raw, first = e_raw[q]
-            grouped = keep.tile([P, EDGE_TILE, PACK], BF16, name="e_grouped%d" % q, align_bytes=64)
-            if vector_columns > 0:
-                cast("vector", raw[:, :, first : first + vector_columns], grouped[:, 0:vector_columns, :])
-            if vector_columns < EDGE_TILE:
-                cast("scalar", raw[:, :, first + vector_columns : first + EDGE_TILE], grouped[:, vector_columns:EDGE_TILE, :])
-            return grouped
+                add_pass(q, weight, picked[:, cols], planes[z][SCALE_ROWS * z : P, cols], first, False)
 
         def edge_pass(q, grouped):
-            e_codes, e_scales = quantize("e%d" % q, grouped)
-            add_pass(q, w3_quantized, e_codes[:], e_scales[:], False, True)
+            codes, scales = quantize("e%d" % q, grouped)
+            add_pass(q, w3_quantized, codes[:], scales[:], False, True)
 
         def relu(q, engine):
-            grouped = keep.tile([P, EDGE_TILE, PACK], BF16, name="h_grouped%d" % q, align_bytes=64)
+            grouped = sbuf("h_grouped%d" % q, [P, EDGE_TILE, PACK], BF16)
             if engine == "scalar":
                 nc.scalar.activation(out=grouped[:], in_=acc[q][:].rearrange("p t v -> p v t"), func=RELU)
             else:
@@ -117,13 +116,13 @@ def tile_picked_edgeup_relu_p_kernel(tc, x_words, x_scales, eT, w1, w2, w3, w4_w
             return grouped
 
         def second_layer(q, grouped, product):
-            h_codes, h_scales = quantize("h%d" % q, grouped)
+            codes, scales = quantize("h%d" % q, grouped)
             nc.tensor.matmul_mx(
                 out=product,
                 lhsT=w4_codes[:].bitcast(FP4X4),
                 lhsT_scale=w4_plane[:],
-                rhs=h_codes[:].bitcast(FP8X4),
-                rhs_scale=h_scales[:],
+                rhs=codes[:].bitcast(FP8X4),
+                rhs_scale=scales[:],
                 start=True,
                 stop=True,
             )
@@ -136,59 +135,52 @@ def tile_picked_edgeup_relu_p_kernel(tc, x_words, x_scales, eT, w1, w2, w3, w4_w
                 column = column + product.shape[1]
             nc.sync.dma_start(out=out[:, EDGE_TILE * first_tile : EDGE_TILE * (first_tile + 2)], in_=result[:])
 
-        node_scales = keep.tile([P, T], U8, name="node_scales", align_bytes=64)
-        nc.vector.memset(node_scales[0:64, :].bitcast(I32), 0)
-        nc.vector.memset(node_scales[96:P, :].bitcast(I32), 0)
-        picked_scales = []
-        for z in range(X_PASSES):
-            plane = keep.tile([P, S], U8, name="picked_scales%d" % z, align_bytes=64)
-            nc.vector.memset(plane[:].bitcast(I32), 0)
-            picked_scales.append(plane)
-
+        node_scales = sbuf("node_scales", [P, T], U8)
+        nc.vector.memset(node_scales[:].bitcast(I32), 0)
         offsets = keep.tile([P, S // 16], U16, name="offsets")
-        nc.sync.dma_start(out=node_scales[64:96, :].bitcast(I32), in_=x_scales.rearrange("z q n -> (z q) n").bitcast(I32))
         nc.sync.dma_start(offsets[:], offs)
-        node_words = keep.tile([P, X_PASSES, T], U32, name="node_words", tag="node_words", align_bytes=64)
-        nc.sync.dma_start(out=node_words[:].bitcast(I32), in_=x_words.rearrange("z p n t -> p z (n t)").bitcast(I32))
-        w1_raw = keep.tile([P, X_PASSES, PACK, H], F32, name="w1_raw", tag="w1_raw", align_bytes=64)
-        nc.sync.dma_start(out=w1_raw[:], in_=w1.rearrange("(z p j) w -> p z j w", z=X_PASSES, j=PACK))
+        nc.sync.dma_start(out=node_scales[0:P:4, :].bitcast(I32), in_=x_scales.rearrange("z q n -> q z n").bitcast(I32))
+        words0 = load_words(0)
+        words1 = load_words(1)
+        w1a_raw = load_rows("w1a_raw", w1[0:K_PASS, :])
+        w1b_raw = load_rows("w1b_raw", w1[K_PASS:K, :])
 
-        picked_rows = keep.tile([P, S], U8, name="picked_rows", align_bytes=64)
+        picked_rows = sbuf("picked_rows", [P, S], U8)
         nc.vector.tensor_copy(picked_rows[:], node_scales[:].indirect(offsets[:]))
-
-        def move_scale_rows(moves):
-            for z, r in moves:
+        planes = [sbuf("plane%d" % z, [P, S], U8) for z in range(X_PASSES)]
+        for plane in planes:
+            nc.vector.tensor_copy(plane[:].bitcast(I32), picked_rows[:].bitcast(I32))
+        for r in range(1, SCALE_ROWS):
+            for z in range(X_PASSES):
                 nc.sync.dma_start(
-                    out=picked_scales[z][4 * z + r : P : 32, :].bitcast(I32),
-                    in_=picked_rows[64 + 16 * z + r : 64 + 16 * (z + 1) : 4, :].bitcast(I32),
+                    out=planes[z][SCALE_ROWS * z + r : P : QUADRANT, :].bitcast(I32),
+                    in_=planes[1 - z][SCALE_ROWS * z + 8 * r : P : QUADRANT, :].bitcast(I32),
                 )
+        w2a_raw = load_rows("w2a_raw", w2[0:K_PASS, :], "picked_rows")
+        picked0 = gather_words(0, words0, "node_scales")
+        w2b_raw = load_rows("w2b_raw", w2[K_PASS:K, :], "node_words0")
+        picked1 = gather_words(1, words1)
+        w3_raw = load_rows("w3_raw", w3, "node_words1")
 
-        move_scale_rows([(0, 0), (1, 0), (0, 1), (1, 1), (0, 2), (0, 3)])
-        w2a_raw = load_rows("w2a_raw", w2[0:K_PASS, :], "node_scales")
-        move_scale_rows([(1, 2), (1, 3)])
-        picked0 = gather_words(0)
-        picked1 = gather_words(1)
-        w2b_raw = load_rows("w2b_raw", w2[K_PASS:K, :], "node_words")
-        node_pass(0, 0, picked0, quantize_weight("w1a", w1_raw[:, 0], 256), True)
-        w1b_grouped = cast_weight("w1b", w1_raw[:, 1], 256)
-        w3_raw = load_rows("w3_raw", w3, "w1a_grouped")
+        node_pass(0, 0, picked0, quantize("w1a", cast_weight("w1a", w1a_raw, 512)), True)
+        e_first = load_rows("e_raw0", eT[:, 0 : 2 * EDGE_TILE], "w1a_grouped")
+        w1b_grouped = cast_weight("w1b", w1b_raw, 320)
+        e_last = load_rows("e_raw1", eT[:, 2 * EDGE_TILE : V], "w1b_raw")
         node_pass(1, 0, picked1, quantize("w1b", w1b_grouped), False)
-        e_first = load_rows("e_raw0", eT[:, 0 : 2 * EDGE_TILE], "w1b_grouped")
-        w2a_grouped = cast_weight("w2a", w2a_raw, 320)
-        e_last = load_rows("e_raw1", eT[:, 2 * EDGE_TILE : V], "node_scales")
         e_raw = [(e_first, 0), (e_first, EDGE_TILE), (e_last, 0), (e_last, EDGE_TILE)]
-        node_pass(0, 1, picked0, quantize("w2a", w2a_grouped), False)
-        w4_codes = keep.tile([P, 2 * N], U8, name="w4_codes", tag="w2a_grouped", align_bytes=64)
+        w2a_grouped = cast_weight("w2a", w2a_raw, 320)
+        w4_codes = sbuf("w4_codes", [P, 2 * N], U8, "picked_rows")
         nc.sync.dma_start(out=w4_codes[:].bitcast(I32), in_=w4_words[0].bitcast(I32))
-        node_pass(1, 1, picked1, quantize_weight("w2b", w2b_raw, 336), False)
-        w4_plane = keep.tile([P, N], U8, name="w4_plane", tag="node_words", align_bytes=64)
+        node_pass(0, 1, picked0, quantize("w2a", w2a_grouped), False)
+        node_pass(1, 1, picked1, quantize("w2b", cast_weight("w2b", w2b_raw, 336)), False)
+        w4_plane = sbuf("w4_plane", [P, N], U8, "node_words0")
         nc.vector.memset(w4_plane[:].bitcast(I32), 0)
-        for q in range(QUADRANTS):
+        for c in range(QUADRANTS):
             nc.sync.dma_start(
-                out=w4_plane[32 * q : 32 * q + 4, :].bitcast(I32),
-                in_=w4_scales[0, 4 * q : 4 * q + 4, :].bitcast(I32),
+                out=w4_plane[QUADRANT * c : QUADRANT * c + SCALE_ROWS, :].bitcast(I32),
+                in_=w4_scales[0, SCALE_ROWS * c : SCALE_ROWS * (c + 1), :].bitcast(I32),
             )
-        w3_quantized = quantize_weight("w3", w3_raw, 192)
+        w3_quantized = quantize("w3", cast_weight("w3", w3_raw, 192))
 
         e0 = cast_edges(0, 0)
         e1 = cast_edges(1, 0)

@@ -127,13 +127,11 @@ def tile_picked_edgeup_relu_p_kernel(tc, x_words, x_scales, eT, w1, w2, w3, w4_w
                 stop=True,
             )
 
-        def store(first_tile, products):
-            result = keep.tile([N, 2 * EDGE_TILE], F32, name="result%d" % first_tile)
-            column = 0
-            for product, engine in products:
-                copy_on(engine, result[:, column : column + product.shape[1]], product[:])
-                column = column + product.shape[1]
-            nc.sync.dma_start(out=out[:, EDGE_TILE * first_tile : EDGE_TILE * (first_tile + 2)], in_=result[:])
+        def store(first_tile, product, engine):
+            width = product.shape[1]
+            result = sbuf("result%d" % first_tile, [N, width], F32)
+            copy_on(engine, result[:], product[:])
+            nc.sync.dma_start(out=out[:, EDGE_TILE * first_tile : EDGE_TILE * first_tile + width], in_=result[:])
 
         node_scales = sbuf("node_scales", [P, T], U8)
         nc.vector.memset(node_scales[:].bitcast(I32), 0)
@@ -142,8 +140,8 @@ def tile_picked_edgeup_relu_p_kernel(tc, x_words, x_scales, eT, w1, w2, w3, w4_w
         nc.sync.dma_start(out=node_scales[0:P:4, :].bitcast(I32), in_=x_scales.rearrange("z q n -> q z n").bitcast(I32))
         words0 = load_words(0)
         words1 = load_words(1)
-        w1a_raw = load_rows("w1a_raw", w1[0:K_PASS, :])
-        w1b_raw = load_rows("w1b_raw", w1[K_PASS:K, :])
+        w1_raw = sbuf("w1_raw", [P, X_PASSES, PACK, H], F32)
+        nc.sync.dma_start(out=w1_raw[:], in_=w1.rearrange("(z p j) w -> p z j w", z=X_PASSES, j=PACK))
 
         picked_rows = sbuf("picked_rows", [P, S], U8)
         nc.vector.tensor_copy(picked_rows[:], node_scales[:].indirect(offsets[:]))
@@ -162,17 +160,18 @@ def tile_picked_edgeup_relu_p_kernel(tc, x_words, x_scales, eT, w1, w2, w3, w4_w
         picked1 = gather_words(1, words1)
         w3_raw = load_rows("w3_raw", w3, "node_words1")
 
-        node_pass(0, 0, picked0, quantize("w1a", cast_weight("w1a", w1a_raw, 512)), True)
+        w1a_grouped = cast_weight("w1a", w1_raw[:, 0], 352)
+        w1b_grouped = cast_weight("w1b", w1_raw[:, 1], 256)
+        node_pass(0, 0, picked0, quantize("w1a", w1a_grouped), True)
         e_first = load_rows("e_raw0", eT[:, 0 : 2 * EDGE_TILE], "w1a_grouped")
-        w1b_grouped = cast_weight("w1b", w1b_raw, 320)
-        e_last = load_rows("e_raw1", eT[:, 2 * EDGE_TILE : V], "w1b_raw")
+        e_last = load_rows("e_raw1", eT[:, 2 * EDGE_TILE : V], "w1_raw")
         node_pass(1, 0, picked1, quantize("w1b", w1b_grouped), False)
         e_raw = [(e_first, 0), (e_first, EDGE_TILE), (e_last, 0), (e_last, EDGE_TILE)]
         w2a_grouped = cast_weight("w2a", w2a_raw, 320)
         w4_codes = sbuf("w4_codes", [P, 2 * N], U8, "picked_rows")
         nc.sync.dma_start(out=w4_codes[:].bitcast(I32), in_=w4_words[0].bitcast(I32))
         node_pass(0, 1, picked0, quantize("w2a", w2a_grouped), False)
-        node_pass(1, 1, picked1, quantize("w2b", cast_weight("w2b", w2b_raw, 336)), False)
+        node_pass(1, 1, picked1, quantize("w2b", cast_weight("w2b", w2b_raw, 304)), False)
         w4_plane = sbuf("w4_plane", [P, N], U8, "node_words0")
         nc.vector.memset(w4_plane[:].bitcast(I32), 0)
         for c in range(QUADRANTS):
@@ -201,5 +200,6 @@ def tile_picked_edgeup_relu_p_kernel(tc, x_words, x_scales, eT, w1, w2, w3, w4_w
         h3 = relu(3, "scalar")
         second_layer(2, h2, p2[:])
         second_layer(3, h3, p3[:])
-        store(0, [(p01, "scalar")])
-        store(2, [(p2, "scalar"), (p3, "vector")])
+        store(0, p01, "scalar")
+        store(2, p2, "scalar")
+        store(3, p3, "vector")

@@ -127,11 +127,12 @@ def tile_picked_edgeup_relu_p_kernel(tc, x_words, x_scales, eT, w1, w2, w3, w4_w
                 stop=True,
             )
 
-        def store(first_tile, product, engine):
-            width = product.shape[1]
-            result = sbuf("result%d" % first_tile, [N, width], F32)
-            copy_on(engine, result[:], product[:])
-            nc.sync.dma_start(out=out[:, EDGE_TILE * first_tile : EDGE_TILE * first_tile + width], in_=result[:])
+        def store(first_tile, engines):
+            result = sbuf("result%d" % first_tile, [N, len(engines), EDGE_TILE], F32)
+            for i, engine in enumerate(engines):
+                copy_on(engine, result[:, i, :], products[first_tile + i][:])
+            columns = slice(EDGE_TILE * first_tile, EDGE_TILE * (first_tile + len(engines)))
+            nc.sync.dma_start(out=out[:, columns], in_=result[:].rearrange("m i v -> m (i v)"))
 
         node_scales = sbuf("node_scales", [P, T], U8)
         nc.vector.memset(node_scales[:].bitcast(I32), 0)
@@ -189,17 +190,15 @@ def tile_picked_edgeup_relu_p_kernel(tc, x_words, x_scales, eT, w1, w2, w3, w4_w
         e3 = cast_edges(3, 0)
         edge_pass(2, e2)
         edge_pass(3, e3)
-        p01 = psum.tile([N, 2 * EDGE_TILE], F32, name="product01")
-        p2 = psum.tile([N, EDGE_TILE], F32, name="product2")
-        p3 = psum.tile([N, EDGE_TILE], F32, name="product3")
+        products = [psum.tile([N, EDGE_TILE], F32, name="product%d" % q) for q in range(EDGE_TILES)]
         h0 = relu(0, "scalar")
-        second_layer(0, h0, p01[:, 0:EDGE_TILE])
+        second_layer(0, h0, products[0][:])
         h1 = relu(1, "scalar")
         h2 = relu(2, "vector")
-        second_layer(1, h1, p01[:, EDGE_TILE : 2 * EDGE_TILE])
+        second_layer(1, h1, products[1][:])
         h3 = relu(3, "scalar")
-        second_layer(2, h2, p2[:])
-        second_layer(3, h3, p3[:])
-        store(0, p01, "scalar")
-        store(2, p2, "scalar")
-        store(3, p3, "vector")
+        second_layer(2, h2, products[2][:])
+        second_layer(3, h3, products[3][:])
+        store(0, ["scalar", "vector"])
+        store(2, ["scalar"])
+        store(3, ["vector"])

@@ -35,7 +35,7 @@ def tile_picked_edgeup_relu_p_kernel(tc, x_words, x_scales, eT, w1, w2, w3, w4_w
         psum = ctx.enter_context(tc.psum_pool(name="psum", bufs=1))
 
         def sbuf(name, shape, dtype, reuses=None):
-            return keep.tile(shape, dtype, name=name, tag=reuses or name, align_bytes=64)
+            return keep.tile(shape, dtype, name=name, tag=reuses or name, align_bytes=256)
 
         def copy_on(engine, dst, src):
             if engine == "scalar":
@@ -136,7 +136,7 @@ def tile_picked_edgeup_relu_p_kernel(tc, x_words, x_scales, eT, w1, w2, w3, w4_w
 
         node_scales = sbuf("node_scales", [P, T], U8)
         nc.vector.memset(node_scales[:].bitcast(I32), 0)
-        offsets = keep.tile([P, S // 16], U16, name="offsets")
+        offsets = keep.tile([P, S // 16], U16, name="offsets", align_bytes=256)
         nc.sync.dma_start(offsets[:], offs)
         nc.sync.dma_start(out=node_scales[0:P:4, :].bitcast(I32), in_=x_scales.rearrange("z q n -> q z n").bitcast(I32))
         words0 = load_words(0)

@@ -101,7 +101,7 @@ def tile_picked_edgeup_relu_p_kernel(tc, x_words, x_scales, eT, w1, w2, w3, w4_w
         def node_pass(z, side, picked, weight, first):
             for q in range(EDGE_TILES):
                 cols = slice(side * V + EDGE_TILE * q, side * V + EDGE_TILE * (q + 1))
-                add_pass(q, weight, picked[:, cols], planes[z][SCALE_ROWS * z : P, cols], first, False)
+                add_pass(q, weight, picked[:, cols], plane[SCALE_ROWS * z : P, cols], first, False)
 
         def edge_pass(q, grouped):
             codes, scales = quantize("e%d" % q, grouped)
@@ -146,14 +146,13 @@ def tile_picked_edgeup_relu_p_kernel(tc, x_words, x_scales, eT, w1, w2, w3, w4_w
 
         picked_rows = sbuf("picked_rows", [P, S], U8)
         nc.vector.tensor_copy(picked_rows[:], node_scales[:].indirect(offsets[:]))
-        planes = [sbuf("plane%d" % z, [P, S], U8) for z in range(X_PASSES)]
-        for plane in planes:
-            nc.vector.tensor_copy(plane[:].bitcast(I32), picked_rows[:].bitcast(I32))
+        plane = sbuf("plane", [P, S], U8)
+        nc.vector.tensor_copy(plane[:].bitcast(I32), picked_rows[:].bitcast(I32))
         for r in range(1, SCALE_ROWS):
             for z in range(X_PASSES):
                 nc.sync.dma_start(
-                    out=planes[z][SCALE_ROWS * z + r : P : QUADRANT, :].bitcast(I32),
-                    in_=planes[1 - z][SCALE_ROWS * z + 8 * r : P : QUADRANT, :].bitcast(I32),
+                    out=plane[SCALE_ROWS * z + r : P : QUADRANT, :].bitcast(I32),
+                    in_=plane[SCALE_ROWS * z + 8 * r : P : QUADRANT, :].bitcast(I32),
                 )
         w2a_raw = load_rows("w2a_raw", w2[0:K_PASS, :], "picked_rows")
         picked0 = gather_words(0, words0, "node_scales")
@@ -161,7 +160,7 @@ def tile_picked_edgeup_relu_p_kernel(tc, x_words, x_scales, eT, w1, w2, w3, w4_w
         picked1 = gather_words(1, words1)
         w3_raw = load_rows("w3_raw", w3, "node_words1")
 
-        w1a_grouped = cast_weight("w1a", w1_raw[:, 0], 352)
+        w1a_grouped = cast_weight("w1a", w1_raw[:, 0], 416)
         w1b_grouped = cast_weight("w1b", w1_raw[:, 1], 256)
         node_pass(0, 0, picked0, quantize("w1a", w1a_grouped), True)
         e_first = load_rows("e_raw0", eT[:, 0 : 2 * EDGE_TILE], "w1a_grouped")

@@ -160,7 +160,7 @@ def tile_picked_edgeup_relu_p_kernel(tc, x_words, x_scales, eT, w1, w2, w3, w4_w
         picked1 = gather_words(1, words1)
         w3_raw = load_rows("w3_raw", w3, "node_words1")
 
-        w1a_grouped = cast_weight("w1a", w1_raw[:, 0], 416)
+        w1a_grouped = cast_weight("w1a", w1_raw[:, 0], 320)
         w1b_grouped = cast_weight("w1b", w1_raw[:, 1], 256)
         node_pass(0, 0, picked0, quantize("w1a", w1a_grouped), True)
         e_first = load_rows("e_raw0", eT[:, 0 : 2 * EDGE_TILE], "w1a_grouped")

from contextlib import ExitStack

import concourse.mybir as mybir

K, T, S, V, H, N, J = 1024, 2048, 1024, 512, 512, 128, 512
FLOPS = 2 * V * H * (2 * K + J) + 2 * V * H * N

F32 = mybir.dt.float32
BF16 = mybir.dt.bfloat16
I32 = mybir.dt.int32
U32 = mybir.dt.uint32
U16 = mybir.dt.uint16
U8 = mybir.dt.uint8
FP8X4 = mybir.dt.float8_e4m3fn_x4
FP4X4 = mybir.dt.float4_e2m1fn_x4
COPY = mybir.ActivationFunctionType.Copy
RELU = mybir.ActivationFunctionType.Relu

P = 128
PACK = 4
K_PASS = P * PACK
X_PASSES = K // K_PASS
EDGE_TILE = 128
EDGE_TILES = V // EDGE_TILE
QUADRANT = 32
QUADRANTS = P // QUADRANT
SCALE_ROWS = 4


def tile_picked_edgeup_relu_p_kernel(tc, x_words, x_scales, eT, w1, w2, w3, w4_words, w4_scales, offs, out):
    nc = tc.nc

    with ExitStack() as ctx:
        keep = ctx.enter_context(tc.tile_pool(name="keep", bufs=1))
        psum = ctx.enter_context(tc.psum_pool(name="psum", bufs=1))

        def sbuf(name, shape, dtype, reuses=None):
            return keep.tile(shape, dtype, name=name, tag=reuses or name, align_bytes=256)

        def copy_on(engine, dst, src):
            if engine == "scalar":
                nc.scalar.activation(out=dst, in_=src, func=COPY)
            else:
                nc.vector.tensor_copy(out=dst, in_=src)

        def load_rows(name, rows, reuses=None):
            raw = sbuf(name, [P, PACK, rows.shape[1]], F32, reuses)
            nc.sync.dma_start(out=raw[:], in_=rows.rearrange("(p j) w -> p j w", j=PACK))
            return raw

        def load_words(z):
            words = sbuf("node_words%d" % z, [P, T], U32)
            nc.sync.dma_start(out=words[:].bitcast(I32), in_=x_words[z].rearrange("p n t -> p (n t)").bitcast(I32))
            return words

        def gather_words(z, words, reuses=None):
            picked = sbuf("picked_words%d" % z, [P, S], U32, reuses)
            nc.vector.tensor_copy(picked[:], words[:].indirect(offsets[:]))
            return picked

        def cast_weight(name, raw, scalar_columns):
            grouped = sbuf(name + "_grouped", [P, H, PACK], BF16)
            for engine, c0, c1 in (("scalar", 0, scalar_columns), ("vector", scalar_columns, H)):
                if c1 > c0:
                    src = raw[:, :, c0:c1].rearrange("p j (m t) -> p m j t", t=PACK)
                    dst = grouped[:].rearrange("p (t m) j -> p m j t", t=PACK)[:, c0 // PACK : c1 // PACK, :, :]
                    copy_on(engine, dst, src)
            return grouped

        def cast_edges(q, vector_columns):
            raw, first = e_raw[q]
            grouped = sbuf("e_grouped%d" % q, [P, EDGE_TILE, PACK], BF16)
            for engine, c0, c1 in (("vector", 0, vector_columns), ("scalar", vector_columns, EDGE_TILE)):
                if c1 > c0:
                    src = raw[:, :, first + c0 : first + c1].rearrange("p j (c i) -> p c j i", i=4)
                    copy_on(engine, grouped[:, c0:c1, :].rearrange("p (c i) j -> p c j i", i=4), src)
            return grouped

        def quantize(name, grouped):
            width = grouped.shape[1]
            codes = sbuf(name + "_codes", [P, width], U32)
            scales = sbuf(name + "_scales", [P, width], U8)
            nc.vector.quantize_mx(out=codes[:].bitcast(FP8X4), scales=scales[:], in_=grouped[:].rearrange("p w j -> p (w j)"))
            return codes, scales

        acc = [psum.tile([P, PACK, EDGE_TILE], F32, name="acc%d" % q) for q in range(EDGE_TILES)]

        def add_pass(q, weight, codes, scales, first, last):
            for t in range(PACK):
                cols = slice(P * t, P * (t + 1))
                nc.tensor.matmul_mx(
                    out=acc[q][:, t, :],
                    lhsT=weight[0][:, cols].bitcast(FP8X4),
                    lhsT_scale=weight[1][:, cols],
                    rhs=codes.bitcast(FP8X4),
                    rhs_scale=scales,
                    start=first and t == 0,
                    stop=last and t == PACK - 1,
                )

        def node_pass(z, side, picked, weight, first):
            for q in range(EDGE_TILES):
                cols = slice(side * V + EDGE_TILE * q, side * V + EDGE_TILE * (q + 1))
                add_pass(q, weight, picked[:, cols], plane[SCALE_ROWS * z : P, cols], first, False)

        def edge_pass(q, grouped):
            codes, scales = quantize("e%d" % q, grouped)
            add_pass(q, w3_quantized, codes[:], scales[:], False, True)

        def relu(q, engine):
            grouped = sbuf("h_grouped%d" % q, [P, EDGE_TILE, PACK], BF16)
            if engine == "scalar":
                nc.scalar.activation(out=grouped[:], in_=acc[q][:].rearrange("p t v -> p v t"), func=RELU)
            else:
                nc.vector.tensor_scalar_max(grouped[:], acc[q][:].rearrange("p t v -> p v t"), 0.0)
            return grouped

        def second_layer(q, grouped, product):
            codes, scales = quantize("h%d" % q, grouped)
            nc.tensor.matmul_mx(
                out=product,
                lhsT=w4_codes[:].bitcast(FP4X4),
                lhsT_scale=w4_plane[:],
                rhs=codes[:].bitcast(FP8X4),
                rhs_scale=scales[:],
                start=True,
                stop=True,
            )

        def store(first_tile, engines):
            result = sbuf("result%d" % first_tile, [N, len(engines), EDGE_TILE], F32)
            for i, engine in enumerate(engines):
                copy_on(engine, result[:, i, :], products[first_tile + i][:])
            columns = slice(EDGE_TILE * first_tile, EDGE_TILE * (first_tile + len(engines)))
            nc.sync.dma_start(out=out[:, columns], in_=result[:].rearrange("m i v -> m (i v)"))

        node_scales = sbuf("node_scales", [P, T], U8)
        nc.vector.memset(node_scales[:].bitcast(I32), 0)
        offsets = keep.tile([P, S // 16], U16, name="offsets", align_bytes=256)
        nc.sync.dma_start(offsets[:], offs)
        nc.sync.dma_start(out=node_scales[0:P:4, :].bitcast(I32), in_=x_scales.rearrange("z q n -> q z n").bitcast(I32))
        words0 = load_words(0)
        words1 = load_words(1)
        w1_raw = sbuf("w1_raw", [P, X_PASSES, PACK, H], F32)
        nc.sync.dma_start(out=w1_raw[:], in_=w1.rearrange("(z p j) w -> p z j w", z=X_PASSES, j=PACK))

        picked_rows = sbuf("picked_rows", [P, S], U8)
        nc.vector.tensor_copy(picked_rows[:], node_scales[:].indirect(offsets[:]))
        plane = sbuf("plane", [P, S], U8)
        nc.vector.tensor_copy(plane[:].bitcast(I32), picked_rows[:].bitcast(I32))
        for r in range(1, SCALE_ROWS):
            for z in range(X_PASSES):
                nc.sync.dma_start(
                    out=plane[SCALE_ROWS * z + r : P : QUADRANT, :].bitcast(I32),
                    in_=plane[SCALE_ROWS * z + 8 * r : P : QUADRANT, :].bitcast(I32),
                )
        w2a_raw = load_rows("w2a_raw", w2[0:K_PASS, :], "picked_rows")
        picked0 = gather_words(0, words0, "node_scales")
        w2b_raw = load_rows("w2b_raw", w2[K_PASS:K, :], "node_words0")
        picked1 = gather_words(1, words1)
        w3_raw = load_rows("w3_raw", w3, "node_words1")

        w1a_grouped = cast_weight("w1a", w1_raw[:, 0], 320)
        w1b_grouped = cast_weight("w1b", w1_raw[:, 1], 256)
        node_pass(0, 0, picked0, quantize("w1a", w1a_grouped), True)
        e_first = load_rows("e_raw0", eT[:, 0 : 2 * EDGE_TILE], "w1a_grouped")
        e_last = load_rows("e_raw1", eT[:, 2 * EDGE_TILE : V], "w1_raw")
        node_pass(1, 0, picked1, quantize("w1b", w1b_grouped), False)
        e_raw = [(e_first, 0), (e_first, EDGE_TILE), (e_last, 0), (e_last, EDGE_TILE)]
        w2a_grouped = cast_weight("w2a", w2a_raw, 320)
        w4_codes = sbuf("w4_codes", [P, 2 * N], U8, "picked_rows")
        nc.sync.dma_start(out=w4_codes[:].bitcast(I32), in_=w4_words[0].bitcast(I32))
        node_pass(0, 1, picked0, quantize("w2a", w2a_grouped), False)
        node_pass(1, 1, picked1, quantize("w2b", cast_weight("w2b", w2b_raw, 304)), False)
        w4_plane = sbuf("w4_plane", [P, N], U8, "node_words0")
        nc.vector.memset(w4_plane[:].bitcast(I32), 0)
        for c in range(QUADRANTS):
            nc.sync.dma_start(
                out=w4_plane[QUADRANT * c : QUADRANT * c + SCALE_ROWS, :].bitcast(I32),
                in_=w4_scales[0, SCALE_ROWS * c : SCALE_ROWS * (c + 1), :].bitcast(I32),
            )
        w3_quantized = quantize("w3", cast_weight("w3", w3_raw, 192))

        e0 = cast_edges(0, 0)
        e1 = cast_edges(1, 0)
        edge_pass(0, e0)
        e2 = cast_edges(2, 128)
        edge_pass(1, e1)
        e3 = cast_edges(3, 0)
        edge_pass(2, e2)
        edge_pass(3, e3)
        products = [psum.tile([N, EDGE_TILE], F32, name="product%d" % q) for q in range(EDGE_TILES)]
        h0 = relu(0, "scalar")
        second_layer(0, h0, products[0][:])
        h1 = relu(1, "scalar")
        h2 = relu(2, "vector")
        second_layer(1, h1, products[1][:])
        h3 = relu(3, "scalar")
        second_layer(2, h2, products[2][:])
        second_layer(3, h3, products[3][:])
        store(0, ["scalar", "vector"])
        store(2, ["scalar"])
        store(3, ["vector"])
